import numpy as np, ml_dtypes
CORES = [66,74,82,90,194,202,210,218]
N = 8
import mx_ref
BF = ml_dtypes.bfloat16
def pick(q, e):
    c = np.concatenate([q[0].reshape(128, -1, 4), np.zeros((128, 1, 4), np.uint8)], axis=1); s = np.concatenate([q[1], np.ones((16, 1), np.uint8)], axis=1)
    return (np.ascontiguousarray(c[:, e].reshape(128, -1)), np.ascontiguousarray(s[:, e]))
def join(*qs):
    return (np.concatenate([q[0] for q in qs], axis=1), np.concatenate([q[1] for q in qs], axis=1))
def put(q, e, v):
    c, s = q[0].reshape(128, -1, 4).copy(), q[1].copy(); c[:, e] = v[0].reshape(128, -1, 4); s[:, e] = v[1]
    return (c.reshape(128, -1), s)
def pk(c, s):
    return (np.ascontiguousarray(c), mx_ref.live(s))
def emit(q):
    return q[0], q[1]
def cols(t, e):
    v = np.concatenate([t.reshape(128, -1, 4), np.zeros((128, 1, 4), BF)], axis=1)
    return np.ascontiguousarray(v[:, e]).reshape(128, -1)
def tile(rs):
    return np.stack(rs, axis=2).reshape(128, -1).astype(BF)
def cut(t, i, w=512):
    return t[:, w * i:w * i + w]
def f(rng, *shape):
    return mx_ref.flush((rng.standard_normal(shape, dtype=np.float32) * np.exp2(rng.integers(-2, 3, shape[:-1] + (1,)))).astype(BF))
def wide(rng, *shape, cols=0):
    v = rng.standard_normal(shape, dtype=np.float32) * np.exp2(rng.integers(-12, 13, shape)).astype(np.float32)
    if cols: v *= np.repeat(np.exp2(rng.integers(-cols, cols + 1, shape[:-2] + (1, shape[-1] // 4))) * (rng.random(shape[:-2] + (1, shape[-1] // 4)) > 0.0625), 4, axis=-1).astype(np.float32)
    return mx_ref.flush(v.astype(BF))
P, K, O = 96, 32, 1
E = P + 2 * K // N
def play(x, u, a, b):
    row = mx_ref.quantize(np.concatenate([x[r] for r in range(N)], axis=1))
    num = 4 * np.arange(N * P)
    k = mx_ref.quantize(np.ascontiguousarray(u[0]))
    high = []
    for t in range(2):
        n = num.size
        s = mx_ref.matmul(k, row)[0] + np.float32(0)
        split = np.sort(np.argsort(-s, kind="stable")[:K])
        parents = pick(row, split)
        kids = []
        for m in (a[0], b[0]):
            kids.append(tile([mx_ref.matmul(mx_ref.quantize(np.ascontiguousarray(cut(m, i))), parents) * np.float32(0.0625) for i in range(4)]))
        size = np.max(np.abs(np.stack(kids).astype(np.float32)).reshape(2, 16, 8, K, 4), axis=(2, 4))
        high.append((np.max(np.abs(s)), np.max(size), np.min(np.where(size == 0, np.float32(1), size))))
        e = np.repeat(np.arange(n), 1 + np.isin(np.arange(n), split))
        first = split + np.arange(K)
        num = num[e]
        num[first + 1] += 2 - t
        e[first] = n + np.arange(K)
        e[first + 1] = n + K + np.arange(K)
        row = pick(join(row, mx_ref.quantize(kids[0]), mx_ref.quantize(kids[1])), e)
    return row, num, high
def times(t, v):
    return mx_ref.flush((t.astype(np.float32) * np.float32(v)).astype(BF))
def lift(d, r, e, v):
    s = np.where(d["u"][0][:, None, :4].astype(np.float32) < 0, -v, v)
    x = np.array(d["x"][r].astype(np.float32)).reshape(128, P, 4)
    x[:, e] = np.abs(x[:, e]) * s
    d["x"][r] = mx_ref.flush(x.reshape(128, -1).astype(BF))
def setup_inputs(rng):
    u = np.array(f(rng, 128, 512))
    u[:, 4:] = 0
    return {"x": np.array(f(rng, N, 128, 4 * P)), "u": np.stack([u] * N), "a": np.stack([f(rng, 128, 2048)] * N), "b": np.stack([f(rng, 128, 2048)] * N), "w": f(rng, N, 128, 512 * O)}
def setup_inputs_below(rng):
    d = setup_inputs(rng)
    d["x"] = np.array(times(d["x"], 2.0 ** 20))
    for r in range(N): lift(d, r, np.arange(P), -1)
    lift(d, N - 1, rng.permutation(P)[:K], -2.0 ** -6)
    v, p = d["a"][0].astype(np.float32) * np.float32(2.0 ** -6), np.arange(128)
    for i in range(4): v[p, 512 * i + 4 * p + i] = 128
    d["a"] = np.stack([mx_ref.flush(v.astype(BF))] * N)
    d["b"] = times(d["a"], 2.0 ** -4)
    return d
def setup_inputs_edge(rng):
    d = setup_inputs(rng)
    d["a"], d["b"], d["x"] = times(d["a"], 2.0 ** -12), times(d["b"], 2.0 ** -12), np.array(times(d["x"], 64))
    lift(d, int(rng.integers(1, N - 1)), rng.permutation(P)[:K], 4096)
    lift(d, N - 1, rng.permutation(P)[:K], 64)
    return d
def setup_inputs_spread(rng):
    return {**setup_inputs(rng), "x": wide(rng, N, 128, 4 * P, cols=6)}
def setup_inputs_ties(rng):
    d = setup_inputs(rng)
    v, e = times(f(rng, 128, 24), 2.0 ** 14), (rng.permutation(N * P) % 6).reshape(N, P)
    d["x"] = np.stack([cols(v, e[r]) for r in range(N)])
    lift(d, N - 1, rng.permutation(P)[:K // 8], 64)
    return {**d, "b": d["a"].copy()}
def setup_inputs_zero(rng):
    d = setup_inputs(rng)
    d["u"][:, 64:] = 0
    for r in range(N):
        kind = rng.permutation(P) % 3
        lift(d, r, np.flatnonzero(kind == 2), -1)
        x = np.array(d["x"][r]).reshape(128, P, 4)
        x[:, kind == 0] = 0
        x[:64, kind == 1] = 0
        d["x"][r] = x.reshape(128, -1)
    return d
def check_inputs(d):
    b = []
    for k in ("x", "u", "a", "b", "w"):
        v = np.abs(d[k].astype(np.float32))
        if not (np.isfinite(v).all() and ((v == 0) | (v >= 2.0 ** -30) & (v <= 2.0 ** 30)).all()): b.append("a value of " + k)
    if (d["u"][:, :, 4:].astype(np.float32) != 0).any(): b.append("u has numbers behind its column 0")
    for k in ("u", "a", "b"):
        v = d[k].astype(np.float32)
        if (v != v[:1]).any(): b.append(k + " differs between ranks")
    if not b:
        try:
            high = play(d["x"], d["u"], d["a"], d["b"])[2]
            if not all(np.isfinite(s) for s, c, m in high): b.append("a score")
            if not all(c <= 2.0 ** 30 and m >= 2.0 ** -30 for s, c, m in high): b.append("a number of a child")
        except Exception:
            b.append("a number of a child")
    return b
def reference(x, u, a, b, w):
    row, num, _ = play(x, u, a, b)
    oc, osc = np.zeros((N, 128, 4 * E), np.uint8), np.zeros((N, 16, E), np.uint8)
    hs, y = np.zeros((N, 1, E), np.float32), np.zeros((N, 128, O * E), np.float32)
    for r in range(N):
        q = pick(row, np.arange(r * E, r * E + E))
        oc[r], osc[r] = emit(q)
        hs[r, 0] = num[r * E:r * E + E]
        for o in range(O):
            y[r, :, o * E:o * E + E] = mx_ref.matmul(mx_ref.quantize(np.ascontiguousarray(cut(w[r], o))), q)
    return {"oc": oc, "osc": osc, "hs": hs, "y": y}

@@ -1,0 +1,412 @@
+import numpy as np
+from concourse.bass import DstId, RemoteDMATransfer
+from concourse.mybir import dt, AluOpType, AxisListType, ActivationFunctionType
+
+N, P, K = 8, 96, 32
+E = P + 2 * K // N
+WN = 168
+BIG = 1048576.0
+HUGE = 1.0e29
+CODE = "float8_e4m3fn_x4"
+
+
+def _sb(n, d="float32"):
+    return ("sbuf", [128, n], d)
+
+
+SCRATCH = {
+    "XT": _sb(512, "bfloat16"), "UC": _sb(4, "bfloat16"), "UT": _sb(512, "bfloat16"), "ZB": _sb(128, "bfloat16"),
+    "AT": _sb(2048, "bfloat16"), "BT": _sb(2048, "bfloat16"), "WT": _sb(512, "bfloat16"),
+    "QX": _sb(128, CODE), "sQX": _sb(128, "uint8"), "QU": _sb(128, CODE), "sQU": _sb(128, "uint8"),
+    "QA": _sb(512, CODE), "sQA": _sb(512, "uint8"), "QB": _sb(512, CODE), "sQB": _sb(512, "uint8"),
+    "QW": _sb(128, CODE), "sQW": _sb(128, "uint8"),
+    "SRC": _sb(7 * WN, CODE), "sSRC": _sb(7 * WN, "uint8"),
+    "KT": _sb(768, "bfloat16"), "QK": _sb(192, CODE), "sQK": _sb(192, "uint8"),
+    "WK": _sb(1344, "bfloat16"), "GA": _sb(1344, "bfloat16"), "GB": _sb(1344, "bfloat16"),
+    "RUN": _sb(128, CODE), "sRUN": _sb(128, "uint8"), "YT": _sb(E),
+    "ps": ("psum", [128, 4096], "float32"),
+    "Z32": _sb(32), "GM": _sb(224), "PI": _sb(1, "int32"), "PM": _sb(2, "int32"), "PF": _sb(1), "X32": _sb(1), "X16": _sb(1),
+    "FI": _sb(128), "XB": _sb(3), "TRI": _sb(288), "JC": _sb(1), "KAP": _sb(1), "KV": _sb(96), "VR": _sb(96), "FC": _sb(1),
+    "PB": _sb(1), "PC": _sb(2), "PN": _sb(2), "PW": _sb(2), "PH": _sb(1), "PH4": _sb(1),
+    "X1S": _sb(1), "X1L": _sb(7), "SROW": _sb(96), "TS": _sb(96), "LG": _sb(288), "LE": _sb(288), "LB": _sb(288), "LP": _sb(3),
+    "Z1": _sb(224), "EX1": _sb(224), "R1": _sb(224), "CM": _sb(672), "J1": _sb(448), "CN": _sb(3), "CA": _sb(6),
+    "U1": _sb(3), "U2": _sb(3), "Z3": _sb(96), "EX3": _sb(96), "PR": _sb(96), "OH": _sb(96), "M1": _sb(96), "M2": _sb(96), "J2": _sb(96),
+    "XS": _sb(2), "X2L": _sb(14), "SC": _sb(2), "Z2": _sb(64), "EX2": _sb(64), "R2": _sb(64), "D": _sb(192),
+    "GE": _sb(192), "EQ": _sb(96), "KL": _sb(96), "P1": _sb(1), "PEN": _sb(1), "EXM": _sb(32), "RM": _sb(32), "MR": _sb(128),
+    "F0": _sb(1), "LT": _sb(128), "RK": _sb(1), "EXF": _sb(32), "RF": _sb(32), "FR": _sb(128),
+    "W0": _sb(384), "W1": _sb(384), "J3": _sb(384), "AC": _sb(2), "OF": _sb(2), "OTF": _sb(8), "OT": _sb(8, "uint16"),
+    "WH": _sb(256), "HA": _sb(1), "HB": _sb(1),
+}
+COUNTERS = ["v", "s", "p", "q"]
+DMAS = ["dx", "du", "da", "db", "dw", "w0", "w1", "w2", "w3", "o0", "o1", "o2", "o3", "o4", "o5", "o6"]
+SEMAPHORES = COUNTERS + DMAS + ["x1", "x2", "halo", "left"]
+F = ActivationFunctionType.Copy
+ADD, SUB, MUL, MIN = AluOpType.add, AluOpType.subtract, AluOpType.mult, AluOpType.min
+GT, GE, LT, LE, EQ = AluOpType.is_gt, AluOpType.is_ge, AluOpType.is_lt, AluOpType.is_le, AluOpType.is_equal
+
+
+def view(name, c0=0, c1=None, p0=0, p1=128, step=1):
+    if c1 is None:
+        c1 = SCRATCH[name][1][1]
+    return (name, p0, p1, c0, c1, step)
+
+
+def meet(a, b):
+    if a[1] >= b[2] or b[1] >= a[2] or a[3] >= b[4] or b[3] >= a[4]:
+        return False
+    return not (a[5] == b[5] and a[5] > 1 and (a[3] - b[3]) % a[5])
+
+
+def holds(a, b):
+    return a[5] == 1 and a[1] <= b[1] and a[2] >= b[2] and a[3] <= b[3] and a[4] >= b[4]
+
+
+def rank_program(g, core, T, topo):
+    r = T.rank_of(core)
+    if r is None:
+        return
+    queues = {"v": g.vector, "s": g.scalar, "p": g.tensor, "q": g, "y": g.sync}
+    total = {}
+    known = {k: {} for k in queues}
+    clocks = {}
+    log = {}
+
+    def ap(w):
+        n, p0, p1, c0, c1, st = w
+        return T[n][p0:p1, c0:c1] if st == 1 else T[n][p0:p1, c0:c1:st]
+
+    def wide(w):
+        if w[0] != "ps":
+            return w
+        return ("ps", 0, 128, w[3] // 512 * 512, (w[4] + 511) // 512 * 512, 1)
+
+    def await_(q, need):
+        for s, n in sorted(need.items()):
+            if known[q].get(s, 0) < n:
+                queues[q].wait_ge(T.sem[s], n)
+                for s2, n2 in clocks.get((s, n), {}).items():
+                    known[q][s2] = max(known[q].get(s2, 0), n2)
+                known[q][s] = n
+
+    def note(sem, n, q, reads, writes):
+        for w, wr in [(x, False) for x in reads] + [(x, True) for x in writes]:
+            w = wide(w)
+            l = log.setdefault(w[0], [])
+            if wr:
+                l[:] = [e for e in l if not holds(w, e[0])]
+            l.append((w, wr, sem, n, q))
+
+    def op(q, fn, reads, writes, sem=None, inc=1, local=True):
+        need = {}
+        for w, wr in [(x, False) for x in reads] + [(x, True) for x in writes]:
+            for e in log.get(w[0], []):
+                other = w[0] == "ps" and e[4] != q
+                if (wr or e[1] or other) and meet(wide(w), e[0]):
+                    need[e[2]] = max(need.get(e[2], 0), e[3])
+        await_(q, need)
+        sem = sem or q
+        ins = fn(queues[q])
+        if local:
+            ins.then_inc(T.sem[sem], inc)
+        total[sem] = total.get(sem, 0) + inc
+        clocks[(sem, total[sem])] = dict(known[q])
+        note(sem, total[sem], q, reads, writes)
+
+    def copy(q, o, i, scale=None):
+        if q == "s":
+            if scale is None:
+                op("s", lambda e: e.activation(ap(o), ap(i), F), [i], [o])
+            else:
+                op("s", lambda e: e.activation(ap(o), ap(i), F, scale=scale), [i], [o])
+        elif scale is None:
+            op("v", lambda e: e.tensor_copy(ap(o), ap(i)), [i], [o])
+        else:
+            op("v", lambda e: e.tensor_scalar(ap(o), ap(i), scale, None, MUL), [i], [o])
+
+    def total_s(o, i, junk):
+        op("s", lambda e: e.activation(ap(junk), ap(i), F, accum_out=ap(o)), [i], [junk, o])
+
+    def total_v(o, i):
+        op("v", lambda e: e.tensor_reduce(ap(o), ap(i), AxisListType.X, ADD), [i], [o])
+
+    def ts(o, i, s1, op0, s2=None, op1=None):
+        rd = [i] + [s for s in (s1, s2) if isinstance(s, tuple)]
+        a1 = ap(s1) if isinstance(s1, tuple) else s1
+        a2 = ap(s2) if isinstance(s2, tuple) else s2
+        if op1 is None:
+            op("v", lambda e: e.tensor_scalar(ap(o), ap(i), a1, None, op0), rd, [o])
+        else:
+            op("v", lambda e: e.tensor_scalar(ap(o), ap(i), a1, a2, op0, op1), rd, [o])
+
+    def tt(o, a, b, o0):
+        op("v", lambda e: e.tensor_tensor(ap(o), ap(a), ap(b), o0), [a, b], [o])
+
+    def fill(o, c):
+        op("v", lambda e: e.memset(ap(o), c), [], [o])
+
+    def turn(o, i):
+        op("v", lambda e: e.transpose(ap(o), ap(i)), [i], [o])
+
+    def spread(o, z, n, p1=128):
+        m, z, o = view("GM", 0, n, 0, p1), view(z, 0, n, 0, p1), view(o, 0, n, 0, p1)
+        op("v", lambda e: e.tensor_tensor_scan(ap(o), ap(m), ap(z), 0.0, MUL, ADD), [m, z], [o])
+
+    def cross(dst, src, n, quarters):
+        k = 0
+        for a in range(quarters):
+            for b in range(4):
+                copy("vs"[k % 2], view(dst, a * n, a * n + n, 32 * b, 32 * b + 32), view(src, 0, n, 32 * a, 32 * a + 32))
+                k += 1
+
+    def quant(dst, c0, n, src, e0=0):
+        o, s, i = view(dst, c0, c0 + n), view("s" + dst, c0, c0 + n), view(src, e0, e0 + 4 * n)
+        op("v", lambda e: e.quantize_mx(ap(o), ap(s), ap(i)), [i], [o, s])
+
+    def mm(bank, w, wc, x, xc, n):
+        o = view("ps", 512 * bank, 512 * bank + n)
+        a, sa, b, sb = view(w, wc, wc + 128), view("s" + w, wc, wc + 128), view(x, xc, xc + n), view("s" + x, xc, xc + n)
+        op("p", lambda e: e.matmul_mx(ap(o), ap(a), ap(sa), ap(b), ap(sb), True, True), [a, sa, b, sb], [o])
+
+    def bank(i, n, p0=0, p1=128, c0=0):
+        return view("ps", 512 * i + c0, 512 * i + c0 + n, p0, p1)
+
+    def load(q, name, dst, n, sem):
+        o = view(dst, 0, n)
+        op(q, lambda e: e.dma_start(ap(o), T[name][:, 0:n]), [], [o], sem, 16)
+
+    def move(q, dst, d0, src, s0, n, s1, s2):
+        o, i, os, is_ = view(dst, d0, d0 + n), view(src, s0, s0 + n), view("s" + dst, d0, d0 + n), view("s" + src, s0, s0 + n)
+        op(q, lambda e: e.dma_start(ap(o).bitcast(dt.uint8), ap(i).bitcast(dt.uint8)), [i], [o], s1, 16)
+        op(q, lambda e: e.dma_start(ap(os), ap(is_)), [is_], [os], s2, 16)
+
+    others = [d for d in range(N) if d != r]
+    where = [topo.addr(T.cores[d], core) for d in others]
+    mask = 0xFFFFFFFF
+    for d in others:
+        mask &= topo.mask(core, T.cores[d])
+    lanes = bin(mask).count("1")
+
+    def to_all(src, land, k, sem):
+        dsts = []
+        for d in others:
+            j = r if r < d else r - 1
+            dsts.append(T[land][:, k * j:k * j + k])
+        tr = RemoteDMATransfer(dst_ids=[DstId(rid=int(a), pnc=int(b)) for a, b in where], dma_engine_mask=mask,
+                               remote_sem=T.sem[sem], srcs=[ap(src)], dsts=dsts, alu_op=0)
+        op("q", lambda e: e.remote_dma_fused([tr], local_sem=T.sem.left), [src], [], "left", lanes, False)
+
+    def to_one(d, dst, d0, s0, n):
+        rid, pid = topo.addr(T.cores[d], core)
+        m = topo.mask(core, T.cores[d])
+        ln = bin(m).count("1")
+        c, s = view("QX", s0, s0 + n), view("sQX", s0, s0 + n)
+        oc, os = T[dst][:, d0:d0 + n].bitcast(dt.uint8), T["s" + dst][:, d0:d0 + n]
+        op("q", lambda e: e.remote_dma(oc, ap(c).bitcast(dt.uint8), T.sem.halo, T.sem.left, pid, rid, m), [c], [], "left", ln, False)
+        op("q", lambda e: e.remote_dma(os, ap(s), T.sem.halo, T.sem.left, pid, rid, m), [s], [], "left", ln, False)
+
+    def arrive(sem, n, writes):
+        total[sem] = n
+        note(sem, n, None, [], writes)
+
+    load("s", "u", "UC", 4, "du")
+    load("y", "x", "XT", 4 * P, "dx")
+    load("y", "a", "AT", 2048, "da")
+    load("s", "b", "BT", 2048, "db")
+    load("y", "w", "WT", 512, "dw")
+    op("q", lambda e: e.iota(T.PI[:], [[0, 1]], 0, 1), [], [view("PI")])
+    op("q", lambda e: e.iota(T.FI[:], [[1, 128]], 0, 0, allow_small_or_imprecise_dtypes=True), [], [view("FI")])
+    fill(view("ZB"), 0.0)
+    fill(view("XT", 4 * P, 512), 0.0)
+    fill(view("GM"), 1.0)
+    fill(view("GM", 0, 224, step=32), 0.0)
+    fill(view("Z1"), 0.0)
+    fill(view("Z32"), 0.0)
+    for t in range(4):
+        ts(view("UT", t, 512, step=4), view("ZB"), view("UC", t, t + 1), ADD)
+    quant("QU", 0, 128, "UT")
+    quant("QX", 0, 128, "XT")
+
+    mm(0, "QX", 0, "QU", 0, 128)
+    mm(1, "QU", 0, "QX", 0, 128)
+    copy("s", view("X1S"), bank(0, 1))
+    copy("v", view("SROW"), bank(1, 96))
+    to_all(view("X1S"), "X1L", 1, "x1")
+    arrive("x1", 7 * lanes, [view("X1L")])
+    if r + 1 < N:
+        to_one(r + 1, "SRC", 0, P - (56 - 8 * r), 56 - 8 * r) if r < 7 and 56 - 8 * r > 0 else None
+    if r > 0:
+        to_one(r - 1, "SRC", WN - 8 * r, 0, 8 * r)
+    lo, hi = (64 - 8 * r, 160 - 8 * r)
+    land = []
+    cnt = 0
+    if r > 0:
+        land += [view("SRC", 0, lo), view("sSRC", 0, lo)]
+        cnt += 2 * bin(topo.mask(T.cores[r - 1], core)).count("1")
+    if r < N - 1:
+        land += [view("SRC", hi, WN), view("sSRC", hi, WN)]
+        cnt += 2 * bin(topo.mask(T.cores[r + 1], core)).count("1")
+    arrive("halo", cnt, land)
+    move("y", "SRC", lo, "QX", 0, P, "w0", "w1")
+    if r == 0:
+        move("y", "SRC", 0, "QX", 0, lo, "w2", "w3")
+    if r == N - 1:
+        move("y", "SRC", hi, "QX", 0, WN - hi, "w2", "w3")
+
+    quant("QA", 0, 512, "AT")
+    for i in range(4):
+        mm(i, "QA", 128 * i, "QX", 0, 128)
+    quant("QB", 0, 512, "BT")
+    for i in range(4):
+        mm(4 + i, "QB", 128 * i, "QX", 0, 128)
+    turn(view("TS"), view("SROW"))
+    op("v", lambda e: e.tensor_scalar(T.PM[:, 0:1], T.PI[:], 31, None, AluOpType.bitwise_and), [view("PI")], [view("PM", 0, 1)])
+    copy("v", view("X32"), view("PM", 0, 1))
+    for b in range(3):
+        ts(view("XB", b, b + 1), view("X32"), 32.0 * b, ADD)
+    for b in range(3):
+        ts(view("TRI", 96 * b, 96 * b + 96), view("FI", 0, 96), view("XB", b, b + 1), LT)
+        ts(view("LG", 96 * b, 96 * b + 96), view("SROW"), view("TS", 32 * b, 32 * b + 1), GT)
+        ts(view("LE", 96 * b, 96 * b + 96), view("SROW"), view("TS", 32 * b, 32 * b + 1), EQ)
+    for i in range(4):
+        copy("s", view("KT", i, 384, step=4), bank(i, 96), 0.0625)
+    tt(view("LB"), view("LE"), view("TRI"), MUL)
+    tt(view("LE"), view("LB"), view("LG"), ADD)
+    for b in range(3):
+        total_v(view("LP", b, b + 1), view("LE", 96 * b, 96 * b + 96))
+    for i in range(4):
+        copy("vs"[i % 2], view("KT", 384 + i, 768, step=4), bank(4 + i, 96), 0.0625)
+    quant("QK", 0, 192, "KT")
+    mm(0, "QU", 0, "QK", 0, 192)
+    copy("v", view("JC"), view("X32"))
+    ts(view("JC", p0=64, p1=96), view("X32", p0=64, p1=96), 32.0, ADD)
+    for a, k in enumerate((1, 3, 1, 2)):
+        fill(view("KAP", p0=32 * a, p1=32 * a + 32), 384.0 * r + k)
+        fill(view("FC", p0=32 * a, p1=32 * a + 32), 1.0 - 0.25 * k)
+    ts(view("KV"), view("FI", 0, 96), 4.0, MUL, view("KAP"), ADD)
+    fill(view("VR", p0=96, p1=128), HUGE)
+    fill(view("Z3"), 0.0)
+    fill(view("Z2"), 0.0)
+    copy("v", view("VR", p0=64, p1=96), view("SROW", p0=64, p1=96))
+    copy("v", view("VR", p0=0, p1=32), bank(0, 96, 0, 32))
+    copy("v", view("VR", p0=32, p1=64), bank(0, 96, 32, 64, 96))
+
+    copy("v", view("Z1", 0, 224, step=32), view("X1L"))
+    spread("EX1", "Z1", 224)
+    turn(view("R1"), view("EX1"))
+    for b in range(3):
+        if r > 0:
+            ts(view("CM", 224 * b, 224 * b + 32 * r), view("R1", 0, 32 * r), view("TS", 32 * b, 32 * b + 1), GE)
+        if r < N - 1:
+            ts(view("CM", 224 * b + 32 * r, 224 * b + 224), view("R1", 32 * r, 224), view("TS", 32 * b, 32 * b + 1), GT)
+        if b < 2:
+            total_s(view("CN", b, b + 1), view("CM", 224 * b, 224 * b + 224), view("J1", 224 * b, 224 * b + 224))
+        else:
+            total_v(view("CN", b, b + 1), view("CM", 224 * b, 224 * b + 224))
+    copy("v", view("CA", 0, 3, 0, 32), view("CN", 0, 3, 32, 64))
+    copy("s", view("CA", 3, 6, 0, 32), view("CN", 0, 3, 64, 96))
+    tt(view("U1", p1=32), view("CN", p1=32), view("LP", p1=32), ADD)
+    tt(view("U2", p1=32), view("CA", 0, 3, 0, 32), view("CA", 3, 6, 0, 32), ADD)
+    tt(view("Z3", 0, 96, 0, 32, 32), view("U1", p1=32), view("U2", p1=32), ADD)
+    spread("EX3", "Z3", 96, 32)
+    turn(view("PR", p1=32), view("EX3", p1=32))
+    for a in (1, 2, 3):
+        copy("vsv"[a - 1], view("PR", p0=32 * a, p1=32 * a + 32), view("PR", p1=32))
+    ts(view("OH"), view("PR"), view("JC"), EQ)
+    tt(view("M2"), view("OH"), view("KV"), MUL)
+    total_s(view("XS", 1, 2), view("M2"), view("J2"))
+    tt(view("M1"), view("OH"), view("VR"), MUL)
+    total_v(view("XS", 0, 1), view("M1"))
+    to_all(view("XS"), "X2L", 2, "x2")
+    arrive("x2", 7 * lanes, [view("X2L")])
+
+    for i in range(4):
+        mm(i, "QA", 128 * i, "SRC", 0, WN)
+    for i in range(4):
+        mm(4 + i, "QB", 128 * i, "SRC", 0, WN)
+    for i in range(8):
+        copy("vs"[i % 2], view("WK", i % 4 + 672 * (i // 4), 672 + 672 * (i // 4), step=4), bank(i, WN), 0.0625)
+    quant("SRC", WN, 2 * WN, "WK")
+    for i in range(4):
+        mm(i, "QA", 128 * i, "SRC", WN, 2 * WN)
+    for i in range(4):
+        mm(4 + i, "QB", 128 * i, "SRC", WN, 2 * WN)
+    op("v", lambda e: e.tensor_scalar(T.PM[:, 1:2], T.PI[:], 15, None, AluOpType.bitwise_and), [view("PI")], [view("PM", 1, 2)])
+    copy("v", view("X16"), view("PM", 1, 2))
+    copy("v", view("PF"), view("PI"))
+    tt(view("PB"), view("PF"), view("X32"), SUB)
+    tt(view("PB"), view("PB"), view("X16"), ADD)
+    for h in range(2):
+        ts(view("PC", h, h + 1), view("PB"), 16.0 * h, ADD, E - 1.0, MIN)
+    ts(view("PW"), view("PC"), 64.0, ADD)
+    ts(view("PC"), view("PC"), float(E * r), ADD)
+    ts(view("PN"), view("PC"), 1.0, ADD)
+    ts(view("PH"), view("PF"), float(E * r), ADD)
+    ts(view("PH4"), view("PH"), 4.0, MUL)
+    for i in range(4):
+        copy("vs"[i % 2], view("GA", i, 1344, step=4), bank(i, 2 * WN), 0.0625)
+    for i in range(4):
+        copy("vs"[i % 2], view("GB", i, 1344, step=4), bank(4 + i, 2 * WN), 0.0625)
+    quant("SRC", 3 * WN, 2 * WN, "GA")
+    quant("SRC", 5 * WN, 2 * WN, "GB")
+    quant("QW", 0, 128, "WT")
+
+    for k in range(2):
+        total_v(view("SC", k, k + 1), view("X2L", k, 14, step=2))
+    tt(view("Z2", 0, 64, step=32), view("SC"), view("XS"), ADD)
+    spread("EX2", "Z2", 64)
+    turn(view("R2"), view("EX2"))
+    cross("D", "R2", 64, 3)
+    sc, mc = view("Z2", 0, 1), view("Z2", 32, 33)
+    for a in range(3):
+        ts(view("EQ", 32 * a, 32 * a + 32), view("D", 64 * a, 64 * a + 32), sc, EQ)
+        ts(view("KL", 32 * a, 32 * a + 32), view("D", 64 * a + 32, 64 * a + 64), mc, LT)
+        ts(view("GE", 32 * a, 32 * a + 32), view("D", 64 * a, 64 * a + 32), sc, GT)
+    tt(view("GE", 96, 192), view("EQ"), view("KL"), MUL)
+    total_v(view("P1"), view("GE"))
+    ts(view("PEN"), view("P1"), float(K), GE, BIG, MUL)
+    ts(view("EXM"), view("Z32"), view("PEN"), ADD, mc, ADD)
+    turn(view("RM"), view("EXM"))
+    cross("MR", "RM", 32, 4)
+    ts(view("F0"), view("EXM", 0, 1), 0.25, MUL, view("FC"), ADD)
+    ts(view("LT"), view("MR"), view("EXM", 0, 1), LT)
+    total_v(view("RK"), view("LT"))
+    ts(view("EXF"), view("Z32"), view("RK"), ADD, view("F0"), ADD)
+    turn(view("RF"), view("EXF"))
+    cross("FR", "RF", 32, 4)
+
+    def weigh(buf, p, pn, wa, wb, count):
+        for c0, c1, k in ((0, 32, 0), (32, 64, 1), (64, 128, 2)):
+            ts(view(buf, c0, c1), view("FR", c0, c1), p, EQ, float(wa[k]), MUL)
+            if wb:
+                ts(view(buf, 128 + c0, 128 + c1), view("FR", c0, c1), pn, EQ, float(wb[k]), MUL)
+        ts(view(buf, 256 if wb else 128, 384 if wb else 256), view("FR"), p, LE, float(count), MUL)
+
+    for h in range(2):
+        buf = "W%d" % h
+        weigh(buf, view("PC", h, h + 1), view("PN", h, h + 1), (4 * WN, 6 * WN, 2 * WN), (3 * WN, 2 * WN, WN), -1)
+        if h == 0:
+            total_s(view("AC", h, h + 1), view(buf), view("J3"))
+        else:
+            total_v(view("AC", h, h + 1), view(buf))
+    tt(view("OF"), view("AC"), view("PW"), ADD)
+    cross("OTF", "OF", 2, 4)
+    copy("v", view("OT"), view("OTF"))
+    op("v", lambda e: e.tensor_copy(T.RUN[:, 0:128].bitcast(dt.uint32), T.SRC[:, 0:7 * WN].bitcast(dt.uint32).indirect(T.OT[:, 0:8])),
+       [view("SRC"), view("OT")], [view("RUN")])
+    op("s", lambda e: e.activation(T.sRUN[:, 0:128], T.sSRC[:, 0:7 * WN].indirect(T.OT[:, 0:8]), F),
+       [view("sSRC"), view("OT")], [view("sRUN")])
+
+    mm(0, "QW", 0, "RUN", 0, 128)
+    copy("s", view("YT"), bank(0, E))
+    op("y", lambda e: e.dma_start(T.oc[:, 0:4 * E], T.RUN[:, 0:E].bitcast(dt.uint8)), [view("RUN", 0, E)], [], "o0", 16)
+    for k in range(4):
+        op("y", lambda e: e.dma_start(T.osc[4 * k:4 * k + 4, 0:E], T.sRUN[32 * k:32 * k + 4, 0:E]),
+           [view("sRUN", 0, E, 32 * k, 32 * k + 4)], [], "o%d" % (1 + k), 16)
+    op("s", lambda e: e.dma_start(T.y[:, 0:E], T.YT[:]), [view("YT")], [], "o5", 16)
+    for c0, c1, k in ((0, 32, 1.0), (32, 64, 3.0), (64, 96, 1.0), (96, 128, 2.0)):
+        ts(view("WH", c0, c1), view("FR", c0, c1), view("PH"), EQ, k, MUL)
+    ts(view("WH", 128, 256), view("FR"), view("PH"), LE, -4.0, MUL)
+    total_v(view("HA"), view("WH"))
+    tt(view("HB"), view("HA"), view("PH4"), ADD)
+    op("y", lambda e: e.dma_start(T.hs[0:1, 0:E], T.HB[0:E, 0:1]), [view("HB", 0, 1, 0, E)], [], "o6", 16)
+    await_("y", total)

@@ -1,10 +1,11 @@
-import numpy as np
 from concourse.bass import DstId, RemoteDMATransfer
 from concourse.mybir import dt, AluOpType, AxisListType, ActivationFunctionType
 
 N, P, K = 8, 96, 32
 E = P + 2 * K // N
-WN = 168
+H0 = 7 * P
+HN = 72
+ALL = 14 * P - 24
 BIG = 1048576.0
 HUGE = 1.0e29
 CODE = "float8_e4m3fn_x4"
@@ -17,32 +18,32 @@ def _sb(n, d="float32"):
 SCRATCH = {
     "XT": _sb(512, "bfloat16"), "UC": _sb(4, "bfloat16"), "UT": _sb(512, "bfloat16"), "ZB": _sb(128, "bfloat16"),
     "AT": _sb(2048, "bfloat16"), "BT": _sb(2048, "bfloat16"), "WT": _sb(512, "bfloat16"),
-    "QX": _sb(128, CODE), "sQX": _sb(128, "uint8"), "QU": _sb(128, CODE), "sQU": _sb(128, "uint8"),
+    "QU": _sb(128, CODE), "sQU": _sb(128, "uint8"),
     "QA": _sb(512, CODE), "sQA": _sb(512, "uint8"), "QB": _sb(512, CODE), "sQB": _sb(512, "uint8"),
     "QW": _sb(128, CODE), "sQW": _sb(128, "uint8"),
-    "SRC": _sb(7 * WN, CODE), "sSRC": _sb(7 * WN, "uint8"),
-    "KT": _sb(768, "bfloat16"), "QK": _sb(192, CODE), "sQK": _sb(192, "uint8"),
-    "WK": _sb(1344, "bfloat16"), "GA": _sb(1344, "bfloat16"), "GB": _sb(1344, "bfloat16"),
+    "SRC": _sb(ALL, CODE), "sSRC": _sb(ALL, "uint8"),
+    "KT": _sb(768, "bfloat16"), "GO": _sb(1536, "bfloat16"), "HK": _sb(672, "bfloat16"), "HG": _sb(1440, "bfloat16"),
     "RUN": _sb(128, CODE), "sRUN": _sb(128, "uint8"), "YT": _sb(E),
     "ps": ("psum", [128, 4096], "float32"),
     "Z32": _sb(32), "GM": _sb(224), "PI": _sb(1, "int32"), "PM": _sb(2, "int32"), "PF": _sb(1), "X32": _sb(1), "X16": _sb(1),
-    "FI": _sb(128), "XB": _sb(3), "TRI": _sb(288), "JC": _sb(1), "KAP": _sb(1), "KV": _sb(96), "VR": _sb(96), "FC": _sb(1),
-    "PB": _sb(1), "PC": _sb(2), "PN": _sb(2), "PW": _sb(2), "PH": _sb(1), "PH4": _sb(1),
-    "X1S": _sb(1), "X1L": _sb(7), "SROW": _sb(96), "TS": _sb(96), "LG": _sb(288), "LE": _sb(288), "LB": _sb(288), "LP": _sb(3),
-    "Z1": _sb(224), "EX1": _sb(224), "R1": _sb(224), "CM": _sb(672), "J1": _sb(448), "CN": _sb(3), "CA": _sb(6),
-    "U1": _sb(3), "U2": _sb(3), "Z3": _sb(96), "EX3": _sb(96), "PR": _sb(96), "OH": _sb(96), "M1": _sb(96), "M2": _sb(96), "J2": _sb(96),
-    "XS": _sb(2), "X2L": _sb(14), "SC": _sb(2), "Z2": _sb(64), "EX2": _sb(64), "R2": _sb(64), "D": _sb(192),
-    "GE": _sb(192), "EQ": _sb(96), "KL": _sb(96), "P1": _sb(1), "PEN": _sb(1), "EXM": _sb(32), "RM": _sb(32), "MR": _sb(128),
-    "F0": _sb(1), "LT": _sb(128), "RK": _sb(1), "EXF": _sb(32), "RF": _sb(32), "FR": _sb(128),
-    "W0": _sb(384), "W1": _sb(384), "J3": _sb(384), "AC": _sb(2), "OF": _sb(2), "OTF": _sb(8), "OT": _sb(8, "uint16"),
-    "WH": _sb(256), "HA": _sb(1), "HB": _sb(1),
+    "FI": _sb(96), "XA": _sb(1), "XB": _sb(3), "TRI": _sb(96), "JC": _sb(1), "KAP": _sb(1), "KV": _sb(96), "VR": _sb(96), "FC": _sb(1),
+    "PA": _sb(1), "PB": _sb(1), "PC": _sb(2), "P2": _sb(2), "PN": _sb(2), "NN": _sb(1), "NS": _sb(2), "H2": _sb(1), "NH": _sb(1),
+    "WC": _sb(16),
+    "X1S": _sb(1), "X1L": _sb(7), "SROW": _sb(96), "SQ": _sb(32), "TS": _sb(96), "OE": _sb(96),
+    "Z1": _sb(224), "EX1": _sb(224), "R1": _sb(224), "CM": _sb(864), "J1": _sb(576), "CN": _sb(3), "CA": _sb(6),
+    "U2": _sb(3), "EX3": _sb(96), "PR": _sb(96), "OH": _sb(96), "M1": _sb(96), "M2": _sb(96), "J2": _sb(96),
+    "XS": _sb(2), "X2L": _sb(14), "SC": _sb(2), "EX2": _sb(64), "R2": _sb(64), "D": _sb(192),
+    "GE": _sb(192), "EQ": _sb(96), "KS": _sb(96), "KL": _sb(96), "P1": _sb(1), "PEN": _sb(1), "EXM": _sb(32), "MR": _sb(128),
+    "F0": _sb(1), "RK": _sb(1), "SB": _sb(2), "EXF": _sb(32), "FR": _sb(128), "J4": _sb(896),
+    "W": _sb(528), "AB": _sb(128), "OF": _sb(2), "OTF": _sb(8), "OT": _sb(8, "uint16"),
+    "WH": _sb(132), "HB": _sb(1),
 }
 COUNTERS = ["v", "s", "p", "q"]
 DMAS = ["dx", "du", "da", "db", "dw", "w0", "w1", "w2", "w3", "o0", "o1", "o2", "o3", "o4", "o5", "o6"]
 SEMAPHORES = COUNTERS + DMAS + ["x1", "x2", "halo", "left"]
-F = ActivationFunctionType.Copy
+AF = ActivationFunctionType
 ADD, SUB, MUL, MIN = AluOpType.add, AluOpType.subtract, AluOpType.mult, AluOpType.min
-GT, GE, LT, LE, EQ = AluOpType.is_gt, AluOpType.is_ge, AluOpType.is_lt, AluOpType.is_le, AluOpType.is_equal
+GT, GE, LT, EQ = AluOpType.is_gt, AluOpType.is_ge, AluOpType.is_lt, AluOpType.is_equal
 
 
 def view(name, c0=0, c1=None, p0=0, p1=128, step=1):
@@ -51,10 +52,16 @@ def view(name, c0=0, c1=None, p0=0, p1=128, step=1):
     return (name, p0, p1, c0, c1, step)
 
 
+def quarter(name, a, c0=0, c1=None):
+    return view(name, c0, c1, 32 * a, 32 * a + 32)
+
+
 def meet(a, b):
     if a[1] >= b[2] or b[1] >= a[2] or a[3] >= b[4] or b[3] >= a[4]:
         return False
-    return not (a[5] == b[5] and a[5] > 1 and (a[3] - b[3]) % a[5])
+    if a[5] == 1 and b[5] == 1:
+        return True
+    return bool(set(range(a[3], a[4], a[5])) & set(range(b[3], b[4], b[5])))
 
 
 def holds(a, b):
@@ -112,31 +119,41 @@ def rank_program(g, core, T, topo):
         clocks[(sem, total[sem])] = dict(known[q])
         note(sem, total[sem], q, reads, writes)
 
+    def val(x):
+        return ap(x) if isinstance(x, tuple) else x
+
+    def act(o, i, func=AF.Copy, bias=None, scale=None, acc=None):
+        kw = {}
+        for k, x in (("bias", bias), ("scale", scale), ("accum_out", acc)):
+            if x is not None:
+                kw[k] = val(x)
+        op("s", lambda e: e.activation(ap(o), ap(i), func, **kw), [i] + [x for x in (bias, scale) if isinstance(x, tuple)],
+           [o] + ([acc] if acc is not None else []))
+
+    def ts(o, i, s1, op0, s2=None, op1=None):
+        rd = [i] + [s for s in (s1, s2) if isinstance(s, tuple)]
+        if op1 is None:
+            op("v", lambda e: e.tensor_scalar(ap(o), ap(i), val(s1), None, op0), rd, [o])
+        else:
+            op("v", lambda e: e.tensor_scalar(ap(o), ap(i), val(s1), val(s2), op0, op1), rd, [o])
+
     def copy(q, o, i, scale=None):
         if q == "s":
-            if scale is None:
-                op("s", lambda e: e.activation(ap(o), ap(i), F), [i], [o])
-            else:
-                op("s", lambda e: e.activation(ap(o), ap(i), F, scale=scale), [i], [o])
+            act(o, i, scale=scale)
         elif scale is None:
             op("v", lambda e: e.tensor_copy(ap(o), ap(i)), [i], [o])
         else:
-            op("v", lambda e: e.tensor_scalar(ap(o), ap(i), scale, None, MUL), [i], [o])
-
-    def total_s(o, i, junk):
-        op("s", lambda e: e.activation(ap(junk), ap(i), F, accum_out=ap(o)), [i], [junk, o])
+            ts(o, i, scale, MUL)
 
     def total_v(o, i):
         op("v", lambda e: e.tensor_reduce(ap(o), ap(i), AxisListType.X, ADD), [i], [o])
 
-    def ts(o, i, s1, op0, s2=None, op1=None):
-        rd = [i] + [s for s in (s1, s2) if isinstance(s, tuple)]
-        a1 = ap(s1) if isinstance(s1, tuple) else s1
-        a2 = ap(s2) if isinstance(s2, tuple) else s2
-        if op1 is None:
-            op("v", lambda e: e.tensor_scalar(ap(o), ap(i), a1, None, op0), rd, [o])
-        else:
-            op("v", lambda e: e.tensor_scalar(ap(o), ap(i), a1, a2, op0, op1), rd, [o])
+    junk = [0]
+
+    def signs(i, bias, acc, scale=1.0):
+        o = view("J4", junk[0], junk[0] + 128)
+        junk[0] += 128
+        act(o, i, AF.Sign, bias=bias, scale=scale, acc=acc)
 
     def tt(o, a, b, o0):
         op("v", lambda e: e.tensor_tensor(ap(o), ap(a), ap(b), o0), [a, b], [o])
@@ -147,23 +164,25 @@ def rank_program(g, core, T, topo):
     def turn(o, i):
         op("v", lambda e: e.transpose(ap(o), ap(i)), [i], [o])
 
-    def spread(o, z, n, p1=128):
-        m, z, o = view("GM", 0, n, 0, p1), view(z, 0, n, 0, p1), view(o, 0, n, 0, p1)
-        op("v", lambda e: e.tensor_tensor_scan(ap(o), ap(m), ap(z), 0.0, MUL, ADD), [m, z], [o])
+    def swap(name, n, engines):
+        copy(engines[0], view(name, n, 2 * n, 64, 128), view(name, 0, n, 0, 64))
+        copy(engines[1], view(name, n, 2 * n, 0, 64), view(name, 0, n, 64, 128))
+        for a in range(4):
+            copy(engines[a % 2], quarter(name, a, 2 * n, 4 * n), quarter(name, a ^ 1, 0, 2 * n))
 
     def cross(dst, src, n, quarters):
         k = 0
         for a in range(quarters):
             for b in range(4):
-                copy("vs"[k % 2], view(dst, a * n, a * n + n, 32 * b, 32 * b + 32), view(src, 0, n, 32 * a, 32 * a + 32))
+                copy("vs"[k % 2], quarter(dst, b, a * n, a * n + n), quarter(src, a, 0, n))
                 k += 1
 
     def quant(dst, c0, n, src, e0=0):
         o, s, i = view(dst, c0, c0 + n), view("s" + dst, c0, c0 + n), view(src, e0, e0 + 4 * n)
         op("v", lambda e: e.quantize_mx(ap(o), ap(s), ap(i)), [i], [o, s])
 
-    def mm(bank, w, wc, x, xc, n):
-        o = view("ps", 512 * bank, 512 * bank + n)
+    def mm(bk, w, wc, x, xc, n):
+        o = view("ps", 512 * bk, 512 * bk + n)
         a, sa, b, sb = view(w, wc, wc + 128), view("s" + w, wc, wc + 128), view(x, xc, xc + n), view("s" + x, xc, xc + n)
         op("p", lambda e: e.matmul_mx(ap(o), ap(a), ap(sa), ap(b), ap(sb), True, True), [a, sa, b, sb], [o])
 
@@ -181,7 +200,7 @@ def rank_program(g, core, T, topo):
 
     others = [d for d in range(N) if d != r]
     where = [topo.addr(T.cores[d], core) for d in others]
-    mask = 0xFFFFFFFF
+    mask = topo.mask(core, T.cores[others[0]])
     for d in others:
         mask &= topo.mask(core, T.cores[d])
     lanes = bin(mask).count("1")
@@ -195,12 +214,12 @@ def rank_program(g, core, T, topo):
                                remote_sem=T.sem[sem], srcs=[ap(src)], dsts=dsts, alu_op=0)
         op("q", lambda e: e.remote_dma_fused([tr], local_sem=T.sem.left), [src], [], "left", lanes, False)
 
-    def to_one(d, dst, d0, s0, n):
+    def to_one(d, d0, s0, n):
         rid, pid = topo.addr(T.cores[d], core)
         m = topo.mask(core, T.cores[d])
         ln = bin(m).count("1")
-        c, s = view("QX", s0, s0 + n), view("sQX", s0, s0 + n)
-        oc, os = T[dst][:, d0:d0 + n].bitcast(dt.uint8), T["s" + dst][:, d0:d0 + n]
+        c, s = view("SRC", s0, s0 + n), view("sSRC", s0, s0 + n)
+        oc, os = T.SRC[:, d0:d0 + n].bitcast(dt.uint8), T.sSRC[:, d0:d0 + n]
         op("q", lambda e: e.remote_dma(oc, ap(c).bitcast(dt.uint8), T.sem.halo, T.sem.left, pid, rid, m), [c], [], "left", ln, False)
         op("q", lambda e: e.remote_dma(os, ap(s), T.sem.halo, T.sem.left, pid, rid, m), [s], [], "left", ln, False)
 
@@ -214,199 +233,219 @@ def rank_program(g, core, T, topo):
     load("s", "b", "BT", 2048, "db")
     load("y", "w", "WT", 512, "dw")
     op("q", lambda e: e.iota(T.PI[:], [[0, 1]], 0, 1), [], [view("PI")])
-    op("q", lambda e: e.iota(T.FI[:], [[1, 128]], 0, 0, allow_small_or_imprecise_dtypes=True), [], [view("FI")])
+    op("q", lambda e: e.iota(T.FI[:], [[1, 96]], 0, 0, allow_small_or_imprecise_dtypes=True), [], [view("FI")])
+    fill(view("Z32"), 0.0)
     fill(view("ZB"), 0.0)
     fill(view("XT", 4 * P, 512), 0.0)
     fill(view("GM"), 1.0)
     fill(view("GM", 0, 224, step=32), 0.0)
     fill(view("Z1"), 0.0)
-    fill(view("Z32"), 0.0)
+    op("v", lambda e: e.tensor_scalar(T.PM[:, 0:1], T.PI[:], 31, None, AluOpType.bitwise_and), [view("PI")], [view("PM", 0, 1)])
+    op("v", lambda e: e.tensor_scalar(T.PM[:, 1:2], T.PI[:], 15, None, AluOpType.bitwise_and), [view("PI")], [view("PM", 1, 2)])
+    copy("v", view("PF"), view("PI"))
+    copy("v", view("X32"), view("PM", 0, 1))
+    copy("v", view("X16"), view("PM", 1, 2))
+    tt(view("PA"), view("PF"), view("X32"), SUB)
+    tt(view("XA"), view("X32"), view("PA"), SUB)
+    tt(view("PB"), view("PA"), view("X16"), ADD)
+    alpha, beta, sigma = (4, 6, 2, 2), (3, 2, 1, 1), (1, 3, 1, 2)
+    for a in range(4):
+        for buf, c, v in (("KAP", 0, 4.0 * P * r + sigma[a]), ("FC", 0, 2.0 - 0.5 * sigma[a] + 127.0), ("WC", 0, 2.0 * P * alpha[a]),
+                          ("WC", 1, 2.0 * P * beta[a]), ("WC", 2, float(sigma[a])), ("WC", 3, -2.0 * P * beta[a])):
+            act(quarter(buf, a, c, c + 1), quarter("Z32", a, 0, 1), bias=v)
     for t in range(4):
         ts(view("UT", t, 512, step=4), view("ZB"), view("UC", t, t + 1), ADD)
     quant("QU", 0, 128, "UT")
-    quant("QX", 0, 128, "XT")
+    quant("SRC", 0, 128, "XT")
 
-    mm(0, "QX", 0, "QU", 0, 128)
-    mm(1, "QU", 0, "QX", 0, 128)
+    mm(0, "SRC", 0, "QU", 0, 128)
+    mm(1, "QU", 0, "SRC", 0, 128)
     copy("s", view("X1S"), bank(0, 1))
     copy("v", view("SROW"), bank(1, 96))
     to_all(view("X1S"), "X1L", 1, "x1")
     arrive("x1", 7 * lanes, [view("X1L")])
-    if r + 1 < N:
-        to_one(r + 1, "SRC", 0, P - (56 - 8 * r), 56 - 8 * r) if r < 7 and 56 - 8 * r > 0 else None
+    if r < N - 1:
+        to_one(r + 1, H0, P - (56 - 8 * r), 56 - 8 * r)
     if r > 0:
-        to_one(r - 1, "SRC", WN - 8 * r, 0, 8 * r)
-    lo, hi = (64 - 8 * r, 160 - 8 * r)
-    land = []
-    cnt = 0
+        to_one(r - 1, H0 + HN - 8 * r, 0, 8 * r)
+    land, cnt = [], 0
     if r > 0:
-        land += [view("SRC", 0, lo), view("sSRC", 0, lo)]
+        land += [view("SRC", H0, H0 + 64 - 8 * r), view("sSRC", H0, H0 + 64 - 8 * r)]
         cnt += 2 * bin(topo.mask(T.cores[r - 1], core)).count("1")
     if r < N - 1:
-        land += [view("SRC", hi, WN), view("sSRC", hi, WN)]
+        land += [view("SRC", H0 + 64 - 8 * r, H0 + HN), view("sSRC", H0 + 64 - 8 * r, H0 + HN)]
         cnt += 2 * bin(topo.mask(T.cores[r + 1], core)).count("1")
     arrive("halo", cnt, land)
-    move("y", "SRC", lo, "QX", 0, P, "w0", "w1")
+    move("y", "SRC", H0 - 56, "SRC", 0, 56, "w0", "w1")
     if r == 0:
-        move("y", "SRC", 0, "QX", 0, lo, "w2", "w3")
+        move("y", "SRC", H0, "SRC", 0, 64, "w2", "w3")
     if r == N - 1:
-        move("y", "SRC", hi, "QX", 0, WN - hi, "w2", "w3")
+        move("y", "SRC", H0 + 8, "SRC", 0, 64, "w2", "w3")
 
+    turn(view("TS"), view("SROW"))
+    for a in range(4):
+        act(quarter("SQ", a), quarter("SROW", a, 32 * (a % 3), 32 * (a % 3) + 32))
     quant("QA", 0, 512, "AT")
     for i in range(4):
-        mm(i, "QA", 128 * i, "QX", 0, 128)
+        mm(i, "QA", 128 * i, "SRC", 0, 128)
     quant("QB", 0, 512, "BT")
     for i in range(4):
-        mm(4 + i, "QB", 128 * i, "QX", 0, 128)
-    turn(view("TS"), view("SROW"))
-    op("v", lambda e: e.tensor_scalar(T.PM[:, 0:1], T.PI[:], 31, None, AluOpType.bitwise_and), [view("PI")], [view("PM", 0, 1)])
-    copy("v", view("X32"), view("PM", 0, 1))
+        mm(4 + i, "QB", 128 * i, "SRC", 0, 128)
+    for i in range(8):
+        copy("s", view("KT", i % 4 + 384 * (i // 4), 384 + 384 * (i // 4), step=4), bank(i, 96), 0.0625)
     for b in range(3):
-        ts(view("XB", b, b + 1), view("X32"), 32.0 * b, ADD)
+        ts(view("XB", b, b + 1), view("XA"), 32.0 * b, ADD)
     for b in range(3):
-        ts(view("TRI", 96 * b, 96 * b + 96), view("FI", 0, 96), view("XB", b, b + 1), LT)
-        ts(view("LG", 96 * b, 96 * b + 96), view("SROW"), view("TS", 32 * b, 32 * b + 1), GT)
-        ts(view("LE", 96 * b, 96 * b + 96), view("SROW"), view("TS", 32 * b, 32 * b + 1), EQ)
-    for i in range(4):
-        copy("s", view("KT", i, 384, step=4), bank(i, 96), 0.0625)
-    tt(view("LB"), view("LE"), view("TRI"), MUL)
-    tt(view("LE"), view("LB"), view("LG"), ADD)
-    for b in range(3):
-        total_v(view("LP", b, b + 1), view("LE", 96 * b, 96 * b + 96))
-    for i in range(4):
-        copy("vs"[i % 2], view("KT", 384 + i, 768, step=4), bank(4 + i, 96), 0.0625)
-    quant("QK", 0, 192, "KT")
-    mm(0, "QU", 0, "QK", 0, 192)
+        s, o = view("TS", 32 * b, 32 * b + 1), 288 * b
+        ts(view("TRI", 32 * b, 32 * b + 32), view("FI", 0, 32), view("XB", b, b + 1), LT)
+        ts(view("OE", 32 * b, 32 * b + 32), view("SQ"), s, EQ)
+        ts(view("CM", o + 224, o + 256), view("SQ"), s, GT)
+        tt(view("CM", o + 256, o + 288), view("OE", 32 * b, 32 * b + 32), view("TRI", 32 * b, 32 * b + 32), MUL)
     copy("v", view("JC"), view("X32"))
-    ts(view("JC", p0=64, p1=96), view("X32", p0=64, p1=96), 32.0, ADD)
-    for a, k in enumerate((1, 3, 1, 2)):
-        fill(view("KAP", p0=32 * a, p1=32 * a + 32), 384.0 * r + k)
-        fill(view("FC", p0=32 * a, p1=32 * a + 32), 1.0 - 0.25 * k)
-    ts(view("KV"), view("FI", 0, 96), 4.0, MUL, view("KAP"), ADD)
-    fill(view("VR", p0=96, p1=128), HUGE)
-    fill(view("Z3"), 0.0)
-    fill(view("Z2"), 0.0)
-    copy("v", view("VR", p0=64, p1=96), view("SROW", p0=64, p1=96))
-    copy("v", view("VR", p0=0, p1=32), bank(0, 96, 0, 32))
-    copy("v", view("VR", p0=32, p1=64), bank(0, 96, 32, 64, 96))
+    ts(quarter("JC", 2), quarter("X32", 2), 32.0, ADD)
+    ts(view("KV"), view("FI"), 4.0, MUL, view("KAP"), ADD)
+    fill(quarter("VR", 3), HUGE)
+    copy("v", quarter("VR", 2), quarter("SROW", 2))
+    quant("SRC", P, 2 * P, "KT")
+    mm(0, "QU", 0, "SRC", P, 2 * P)
+    copy("v", quarter("VR", 0), bank(0, 96, 0, 32))
+    copy("v", quarter("VR", 1), bank(0, 96, 32, 64, 96))
+    for i in range(4):
+        mm(1 + i, "QA", 128 * i, "SRC", P, 2 * P)
+    for i in range(4):
+        mm((5 + i) % 8, "QB", 128 * i, "SRC", P, 2 * P)
+    for i in range(4):
+        copy("s", view("GO", i, 768, step=4), bank(1 + i, 192), 0.0625)
 
     copy("v", view("Z1", 0, 224, step=32), view("X1L"))
-    spread("EX1", "Z1", 224)
+    op("v", lambda e: e.tensor_tensor_scan(T.EX1[:], T.GM[:], T.Z1[:], 0.0, MUL, ADD), [view("GM"), view("Z1")], [view("EX1")])
     turn(view("R1"), view("EX1"))
     for b in range(3):
+        s, o = view("TS", 32 * b, 32 * b + 1), 288 * b
         if r > 0:
-            ts(view("CM", 224 * b, 224 * b + 32 * r), view("R1", 0, 32 * r), view("TS", 32 * b, 32 * b + 1), GE)
+            ts(view("CM", o, o + 32 * r), view("R1", 0, 32 * r), s, GE)
         if r < N - 1:
-            ts(view("CM", 224 * b + 32 * r, 224 * b + 224), view("R1", 32 * r, 224), view("TS", 32 * b, 32 * b + 1), GT)
+            ts(view("CM", o + 32 * r, o + 224), view("R1", 32 * r, 224), s, GT)
         if b < 2:
-            total_s(view("CN", b, b + 1), view("CM", 224 * b, 224 * b + 224), view("J1", 224 * b, 224 * b + 224))
+            act(view("J1", o, o + 288), view("CM", o, o + 288), acc=view("CN", b, b + 1))
         else:
-            total_v(view("CN", b, b + 1), view("CM", 224 * b, 224 * b + 224))
-    copy("v", view("CA", 0, 3, 0, 32), view("CN", 0, 3, 32, 64))
-    copy("s", view("CA", 3, 6, 0, 32), view("CN", 0, 3, 64, 96))
-    tt(view("U1", p1=32), view("CN", p1=32), view("LP", p1=32), ADD)
-    tt(view("U2", p1=32), view("CA", 0, 3, 0, 32), view("CA", 3, 6, 0, 32), ADD)
-    tt(view("Z3", 0, 96, 0, 32, 32), view("U1", p1=32), view("U2", p1=32), ADD)
-    spread("EX3", "Z3", 96, 32)
-    turn(view("PR", p1=32), view("EX3", p1=32))
+            total_v(view("CN", b, b + 1), view("CM", o, o + 288))
+    copy("v", quarter("CA", 0, 0, 3), quarter("CN", 1))
+    copy("s", quarter("CA", 0, 3, 6), quarter("CN", 2))
+    tt(quarter("U2", 0), quarter("CA", 0, 0, 3), quarter("CA", 0, 3, 6), ADD)
+    for b in range(3):
+        ts(quarter("EX3", 0, 32 * b, 32 * b + 32), quarter("Z32", 0), quarter("CN", 0, b, b + 1), ADD, quarter("U2", 0, b, b + 1), ADD)
+    turn(quarter("PR", 0), quarter("EX3", 0))
     for a in (1, 2, 3):
-        copy("vsv"[a - 1], view("PR", p0=32 * a, p1=32 * a + 32), view("PR", p1=32))
+        copy("vsv"[a - 1], quarter("PR", a), quarter("PR", 0))
     ts(view("OH"), view("PR"), view("JC"), EQ)
     tt(view("M2"), view("OH"), view("KV"), MUL)
-    total_s(view("XS", 1, 2), view("M2"), view("J2"))
+    act(view("J2"), view("M2"), acc=view("XS", 1, 2))
     tt(view("M1"), view("OH"), view("VR"), MUL)
     total_v(view("XS", 0, 1), view("M1"))
     to_all(view("XS"), "X2L", 2, "x2")
     arrive("x2", 7 * lanes, [view("X2L")])
 
     for i in range(4):
-        mm(i, "QA", 128 * i, "SRC", 0, WN)
+        mm(1 + i, "QA", 128 * i, "SRC", H0 - 56, 128)
     for i in range(4):
-        mm(4 + i, "QB", 128 * i, "SRC", 0, WN)
+        copy("vs"[i % 2], view("GO", 768 + i, 1536, step=4), bank((5 + i) % 8, 192), 0.0625)
+    for i in range(4):
+        mm((5 + i) % 8, "QB", 128 * i, "SRC", H0 - 56, 128)
+    fill(view("HK", 4 * HN, 4 * P), 0.0)
+    fill(view("HG", 4 * 168, 4 * 192), 0.0)
     for i in range(8):
-        copy("vs"[i % 2], view("WK", i % 4 + 672 * (i // 4), 672 + 672 * (i // 4), step=4), bank(i, WN), 0.0625)
-    quant("SRC", WN, 2 * WN, "WK")
-    for i in range(4):
-        mm(i, "QA", 128 * i, "SRC", WN, 2 * WN)
-    for i in range(4):
-        mm(4 + i, "QB", 128 * i, "SRC", WN, 2 * WN)
-    op("v", lambda e: e.tensor_scalar(T.PM[:, 1:2], T.PI[:], 15, None, AluOpType.bitwise_and), [view("PI")], [view("PM", 1, 2)])
-    copy("v", view("X16"), view("PM", 1, 2))
-    copy("v", view("PF"), view("PI"))
-    tt(view("PB"), view("PF"), view("X32"), SUB)
-    tt(view("PB"), view("PB"), view("X16"), ADD)
+        e0 = 4 * P * (i // 4)
+        copy("vs"[i % 2], view("HK", e0 + i % 4, e0 + 4 * HN, step=4), bank((1 + i) % 8, HN, c0=56), 0.0625)
+    quant("SRC", H0 + P, P + HN, "HK")
+    for i in range(8):
+        mm((1 + i) % 8, "QA" if i < 4 else "QB", 128 * (i % 4), "SRC", H0 + P, P + HN)
+    quant("SRC", 3 * P, 4 * P, "GO")
     for h in range(2):
         ts(view("PC", h, h + 1), view("PB"), 16.0 * h, ADD, E - 1.0, MIN)
-    ts(view("PW"), view("PC"), 64.0, ADD)
-    ts(view("PC"), view("PC"), float(E * r), ADD)
-    ts(view("PN"), view("PC"), 1.0, ADD)
-    ts(view("PH"), view("PF"), float(E * r), ADD)
-    ts(view("PH4"), view("PH"), 4.0, MUL)
-    for i in range(4):
-        copy("vs"[i % 2], view("GA", i, 1344, step=4), bank(i, 2 * WN), 0.0625)
-    for i in range(4):
-        copy("vs"[i % 2], view("GB", i, 1344, step=4), bank(4 + i, 2 * WN), 0.0625)
-    quant("SRC", 3 * WN, 2 * WN, "GA")
-    quant("SRC", 5 * WN, 2 * WN, "GB")
+    swap("WC", 4, "ss")
+    act(view("P2"), view("PC"), bias=2.0 * E * r, scale=2.0)
+    act(view("PN"), view("PC"), bias=2.0 * E * r + 2.0, scale=2.0)
+    act(view("NN"), view("PC", 1, 2), bias=-2.0 * E * r - 2.0, scale=-2.0)
+    act(view("NS"), view("PC"), bias=-2.0 * E * r - 1.0, scale=-2.0)
+    act(view("W", 256, 528, step=264), view("PC"), bias=2.0 * E * r - 128.0 - 2.0 * P * r, scale=2.0)
+    act(view("W", 260, 528, step=264), view("PC"), bias=2.0 * E * r - 128.0 - 2.0 * P * (r + 1), scale=2.0)
+    act(view("H2"), view("PF"), bias=2.0 * E * r, scale=2.0)
+    act(view("NH"), view("PF"), bias=-2.0 * E * r - 1.0, scale=-2.0)
+    act(view("WH", 128, 129), view("PF"), bias=4.0 * E * r - 256.0, scale=4.0)
+    fill(view("W", 258, 528, step=264), 0.0)
+    fill(view("W", 259, 528, step=264), 0.0)
     quant("QW", 0, 128, "WT")
+    for i in range(8):
+        e0 = 4 * 192 * (i // 4)
+        copy("vs"[i % 2], view("HG", e0 + i % 4, e0 + 4 * 168, step=4), bank((1 + i) % 8, 168), 0.0625)
+    quant("SRC", H0 + 3 * P, 360, "HG")
 
     for k in range(2):
         total_v(view("SC", k, k + 1), view("X2L", k, 14, step=2))
-    tt(view("Z2", 0, 64, step=32), view("SC"), view("XS"), ADD)
-    spread("EX2", "Z2", 64)
+    for k in (1, 0):
+        ts(view("EX2", 32 * k, 32 * k + 32), view("Z32"), view("SC", k, k + 1), ADD, view("XS", k, k + 1), ADD)
     turn(view("R2"), view("EX2"))
     cross("D", "R2", 64, 3)
-    sc, mc = view("Z2", 0, 1), view("Z2", 32, 33)
+    sc, mc = view("EX2", 0, 1), view("EX2", 32, 33)
     for a in range(3):
         ts(view("EQ", 32 * a, 32 * a + 32), view("D", 64 * a, 64 * a + 32), sc, EQ)
-        ts(view("KL", 32 * a, 32 * a + 32), view("D", 64 * a + 32, 64 * a + 64), mc, LT)
+        act(view("KS", 32 * a, 32 * a + 32), view("D", 64 * a + 32, 64 * a + 64), AF.Sign, bias=mc, scale=-1.0)
+    act(view("KL"), view("KS"), AF.Relu)
+    for a in range(3):
         ts(view("GE", 32 * a, 32 * a + 32), view("D", 64 * a, 64 * a + 32), sc, GT)
     tt(view("GE", 96, 192), view("EQ"), view("KL"), MUL)
     total_v(view("P1"), view("GE"))
     ts(view("PEN"), view("P1"), float(K), GE, BIG, MUL)
     ts(view("EXM"), view("Z32"), view("PEN"), ADD, mc, ADD)
-    turn(view("RM"), view("EXM"))
-    cross("MR", "RM", 32, 4)
-    ts(view("F0"), view("EXM", 0, 1), 0.25, MUL, view("FC"), ADD)
-    ts(view("LT"), view("MR"), view("EXM", 0, 1), LT)
-    total_v(view("RK"), view("LT"))
+    turn(view("MR", 0, 32), view("EXM"))
+    swap("MR", 32, "vs")
+    signs(view("MR"), view("EXM", 0, 1), view("RK"), -1.0)
+    ts(view("F0"), view("EXM", 0, 1), 0.5, MUL, view("FC"), ADD)
+    if r > 0:
+        signs(view("MR"), 4.0 * P * r - 0.5, view("SB", 0, 1), -1.0)
+    if r < N - 1:
+        signs(view("MR"), 4.0 * P * (r + 1) - 0.5, view("SB", 1, 2), -1.0)
     ts(view("EXF"), view("Z32"), view("RK"), ADD, view("F0"), ADD)
-    turn(view("RF"), view("EXF"))
-    cross("FR", "RF", 32, 4)
-
-    def weigh(buf, p, pn, wa, wb, count):
-        for c0, c1, k in ((0, 32, 0), (32, 64, 1), (64, 128, 2)):
-            ts(view(buf, c0, c1), view("FR", c0, c1), p, EQ, float(wa[k]), MUL)
-            if wb:
-                ts(view(buf, 128 + c0, 128 + c1), view("FR", c0, c1), pn, EQ, float(wb[k]), MUL)
-        ts(view(buf, 256 if wb else 128, 384 if wb else 256), view("FR"), p, LE, float(count), MUL)
+    turn(view("FR", 0, 32), view("EXF"))
+    swap("FR", 32, "vs")
 
     for h in range(2):
-        buf = "W%d" % h
-        weigh(buf, view("PC", h, h + 1), view("PN", h, h + 1), (4 * WN, 6 * WN, 2 * WN), (3 * WN, 2 * WN, WN), -1)
-        if h == 0:
-            total_s(view("AC", h, h + 1), view(buf), view("J3"))
-        else:
-            total_v(view("AC", h, h + 1), view(buf))
-    tt(view("OF"), view("AC"), view("PW"), ADD)
+        signs(view("FR"), view("NS", h, h + 1), view("W", 264 * h + 257, 264 * h + 258))
+    act(view("AB"), view("FR"), AF.Abs, bias=view("NN"))
+    for k in range(4):
+        c = 264 + 128 + 32 * k
+        act(view("W", c, c + 32), view("AB", 32 * k, 32 * k + 32), AF.Relu, bias=view("WC", 4 * k + 1, 4 * k + 2), scale=view("WC", 4 * k + 3, 4 * k + 4))
+    if r > 0:
+        ts(view("W", 258, 528, step=264), view("W", 256, 528, step=264), view("SB", 0, 1), LT, 2.0 * (H0 + 64 - 8 * r), MUL)
+    if r < N - 1:
+        ts(view("W", 259, 528, step=264), view("W", 260, 528, step=264), view("SB", 1, 2), GE, 2.0 * (H0 - 32 - 8 * r), MUL)
+    for h in range(2):
+        for k in range(4):
+            f, c = view("FR", 32 * k, 32 * k + 32), 264 * h + 32 * k
+            ts(view("W", c, c + 32), f, view("P2", h, h + 1), EQ, view("WC", 4 * k, 4 * k + 1), MUL)
+            if h == 0:
+                ts(view("W", c + 128, c + 160), f, view("PN", h, h + 1), EQ, view("WC", 4 * k + 1, 4 * k + 2), MUL)
+    for h in range(2):
+        total_v(view("OF", h, h + 1), view("W", 264 * h, 264 * h + 260))
     cross("OTF", "OF", 2, 4)
-    copy("v", view("OT"), view("OTF"))
-    op("v", lambda e: e.tensor_copy(T.RUN[:, 0:128].bitcast(dt.uint32), T.SRC[:, 0:7 * WN].bitcast(dt.uint32).indirect(T.OT[:, 0:8])),
+    ts(view("OT"), view("OTF"), 0.5, MUL)
+    op("v", lambda e: e.tensor_copy(T.RUN[:, 0:128].bitcast(dt.uint32), T.SRC[:, 0:ALL].bitcast(dt.uint32).indirect(T.OT[:, 0:8])),
        [view("SRC"), view("OT")], [view("RUN")])
-    op("s", lambda e: e.activation(T.sRUN[:, 0:128], T.sSRC[:, 0:7 * WN].indirect(T.OT[:, 0:8]), F),
+    op("s", lambda e: e.activation(T.sRUN[:, 0:128], T.sSRC[:, 0:ALL].indirect(T.OT[:, 0:8]), AF.Copy),
        [view("sSRC"), view("OT")], [view("sRUN")])
 
     mm(0, "QW", 0, "RUN", 0, 128)
+    for k in (129, 130):
+        signs(view("FR"), view("NH"), view("WH", k, k + 1))
     copy("s", view("YT"), bank(0, E))
+    op("s", lambda e: e.dma_start(T.y[:, 0:E], T.YT[:]), [view("YT")], [], "o5", 16)
     op("y", lambda e: e.dma_start(T.oc[:, 0:4 * E], T.RUN[:, 0:E].bitcast(dt.uint8)), [view("RUN", 0, E)], [], "o0", 16)
     for k in range(4):
-        op("y", lambda e: e.dma_start(T.osc[4 * k:4 * k + 4, 0:E], T.sRUN[32 * k:32 * k + 4, 0:E]),
+        op("yyss"[k], lambda e: e.dma_start(T.osc[4 * k:4 * k + 4, 0:E], T.sRUN[32 * k:32 * k + 4, 0:E]),
            [view("sRUN", 0, E, 32 * k, 32 * k + 4)], [], "o%d" % (1 + k), 16)
-    op("s", lambda e: e.dma_start(T.y[:, 0:E], T.YT[:]), [view("YT")], [], "o5", 16)
-    for c0, c1, k in ((0, 32, 1.0), (32, 64, 3.0), (64, 96, 1.0), (96, 128, 2.0)):
-        ts(view("WH", c0, c1), view("FR", c0, c1), view("PH"), EQ, k, MUL)
-    ts(view("WH", 128, 256), view("FR"), view("PH"), LE, -4.0, MUL)
-    total_v(view("HA"), view("WH"))
-    tt(view("HB"), view("HA"), view("PH4"), ADD)
+    for k in range(4):
+        ts(view("WH", 32 * k, 32 * k + 32), view("FR", 32 * k, 32 * k + 32), view("H2"), EQ, view("WC", 4 * k + 2, 4 * k + 3), MUL)
+    total_v(view("HB"), view("WH", 0, 131))
     op("y", lambda e: e.dma_start(T.hs[0:1, 0:E], T.HB[0:E, 0:1]), [view("HB", 0, 1, 0, E)], [], "o6", 16)
     await_("y", total)

@@ -9,6 +9,8 @@ ALL = 14 * P - 24
 BIG = 1048576.0
 HUGE = 1.0e29
 CODE = "float8_e4m3fn_x4"
+HALF = "bfloat16"
+CYCLE, SYNC, OWN, FLY, LOCAL = 0.0009, 0.16, 0.14, 1.6, 2.0
 
 
 def _sb(n, d="float32"):
@@ -16,34 +18,34 @@ def _sb(n, d="float32"):
 
 
 SCRATCH = {
-    "XT": _sb(512, "bfloat16"), "UC": _sb(4, "bfloat16"), "UT": _sb(512, "bfloat16"), "ZB": _sb(128, "bfloat16"),
-    "AT": _sb(2048, "bfloat16"), "BT": _sb(2048, "bfloat16"), "WT": _sb(512, "bfloat16"),
+    "XT": _sb(512, HALF), "UC": _sb(4, HALF), "UT": _sb(512, HALF), "ZB": _sb(128, HALF),
+    "AT": _sb(2048, HALF), "BT": _sb(2048, HALF), "WT": _sb(512, HALF),
     "QU": _sb(128, CODE), "sQU": _sb(128, "uint8"),
     "QA": _sb(512, CODE), "sQA": _sb(512, "uint8"), "QB": _sb(512, CODE), "sQB": _sb(512, "uint8"),
     "QW": _sb(128, CODE), "sQW": _sb(128, "uint8"),
     "SRC": _sb(ALL, CODE), "sSRC": _sb(ALL, "uint8"),
-    "KT": _sb(768, "bfloat16"), "GO": _sb(1536, "bfloat16"), "HK": _sb(672, "bfloat16"), "HG": _sb(1440, "bfloat16"),
+    "KT": _sb(768, HALF), "GO": _sb(1536, HALF), "HK": _sb(672, HALF), "HG": _sb(1440, HALF),
     "RUN": _sb(128, CODE), "sRUN": _sb(128, "uint8"), "YT": _sb(E),
     "ps": ("psum", [128, 4096], "float32"),
-    "Z32": _sb(32), "GM": _sb(224), "PI": _sb(1, "int32"), "PM": _sb(2, "int32"), "PF": _sb(1), "X32": _sb(1), "X16": _sb(1),
+    "Z32": _sb(32), "PI": _sb(1, "int32"), "PM": _sb(2, "int32"), "PF": _sb(1), "X32": _sb(1), "X16": _sb(1),
     "FI": _sb(96), "XA": _sb(1), "XB": _sb(3), "TRI": _sb(96), "JC": _sb(1), "KAP": _sb(1), "KV": _sb(96), "VR": _sb(96), "FC": _sb(1),
     "PA": _sb(1), "PB": _sb(1), "PC": _sb(2), "P2": _sb(2), "PN": _sb(2), "NN": _sb(1), "NS": _sb(2), "H2": _sb(1), "NH": _sb(1),
-    "WC": _sb(16),
+    "WC": _sb(16), "THR": _sb(32),
     "X1S": _sb(1), "X1L": _sb(7), "SROW": _sb(96), "SQ": _sb(32), "TS": _sb(96), "OE": _sb(96),
-    "Z1": _sb(224), "EX1": _sb(224), "R1": _sb(224), "CM": _sb(864), "J1": _sb(576), "CN": _sb(3), "CA": _sb(6),
-    "U2": _sb(3), "EX3": _sb(96), "PR": _sb(96), "OH": _sb(96), "M1": _sb(96), "M2": _sb(96), "J2": _sb(96),
-    "XS": _sb(2), "X2L": _sb(14), "SC": _sb(2), "EX2": _sb(64), "R2": _sb(64), "D": _sb(192),
-    "GE": _sb(192), "EQ": _sb(96), "KS": _sb(96), "KL": _sb(96), "P1": _sb(1), "PEN": _sb(1), "EXM": _sb(32), "MR": _sb(128),
-    "F0": _sb(1), "RK": _sb(1), "SB": _sb(2), "EXF": _sb(32), "FR": _sb(128), "J4": _sb(896),
-    "W": _sb(528), "AB": _sb(128), "OF": _sb(2), "OTF": _sb(8), "OT": _sb(8, "uint16"),
+    "EX1": _sb(224), "R1": _sb(224), "CM": _sb(864, HALF), "CN": _sb(432, HALF), "CA": _sb(6),
+    "E0": _sb(96), "EX3": _sb(96), "PR": _sb(96), "OH": _sb(96), "M1": _sb(96), "M2": _sb(96),
+    "XS": _sb(2), "X2L": _sb(14), "SC": _sb(2), "EX2": _sb(64), "DS": _sb(128), "DN": _sb(128), "SG": _sb(128, HALF), "LO": _sb(128, HALF),
+    "BF": _sb(128), "P1": _sb(1), "EXM": _sb(32), "MR": _sb(128),
+    "F0": _sb(1), "RK": _sb(1), "SB": _sb(2), "EXF": _sb(32), "FR": _sb(128), "J4": _sb(2048),
+    "W": _sb(528), "AB": _sb(128), "OF": _sb(260), "OTF": _sb(8), "OT": _sb(8, "uint16"),
     "WH": _sb(132), "HB": _sb(1),
 }
 COUNTERS = ["v", "s", "p", "q"]
 DMAS = ["dx", "du", "da", "db", "dw", "w0", "w1", "w2", "w3", "o0", "o1", "o2", "o3", "o4", "o5", "o6"]
 SEMAPHORES = COUNTERS + DMAS + ["x1", "x2", "halo", "left"]
 AF = ActivationFunctionType
-ADD, SUB, MUL, MIN = AluOpType.add, AluOpType.subtract, AluOpType.mult, AluOpType.min
-GT, GE, LT, EQ = AluOpType.is_gt, AluOpType.is_ge, AluOpType.is_lt, AluOpType.is_equal
+ADD, SUB, MUL, MIN, MAX = AluOpType.add, AluOpType.subtract, AluOpType.mult, AluOpType.min, AluOpType.max
+GT, GE, LT, LE, EQ = AluOpType.is_gt, AluOpType.is_ge, AluOpType.is_lt, AluOpType.is_le, AluOpType.is_equal
 
 
 def view(name, c0=0, c1=None, p0=0, p1=128, step=1):
@@ -52,8 +54,12 @@ def view(name, c0=0, c1=None, p0=0, p1=128, step=1):
     return (name, p0, p1, c0, c1, step)
 
 
-def quarter(name, a, c0=0, c1=None):
-    return view(name, c0, c1, 32 * a, 32 * a + 32)
+def quarter(name, a, c0=0, c1=None, step=1):
+    return view(name, c0, c1, 32 * a, 32 * a + 32, step)
+
+
+def width(w):
+    return len(range(w[3], w[4], w[5]))
 
 
 def meet(a, b):
@@ -68,135 +74,191 @@ def holds(a, b):
     return a[5] == 1 and a[1] <= b[1] and a[2] >= b[2] and a[3] <= b[3] and a[4] >= b[4]
 
 
+def wide(w):
+    if w[0] != "ps":
+        return w
+    return ("ps", 0, 128, w[3] // 512 * 512, (w[4] + 511) // 512 * 512, 1)
+
+
+def accesses(o):
+    return [(w, False) for w in o["rd"]] + [(w, True) for w in o["wr"]]
+
+
+def place(ops):
+    n, log = len(ops), {}
+    before = [dict() for _ in ops]
+    last = None
+    for i, o in enumerate(ops):
+        for w, wr in accesses(o):
+            for v, vr, j in log.get(w[0], []):
+                if j != i and (wr or vr or w[0] == "ps") and meet(wide(w), v):
+                    before[i].setdefault(j, 0.0)
+        if "behind" in o:
+            before[i][o["behind"]] = 0.0
+        if o["qs"] == "q":
+            if last is not None:
+                before[i].setdefault(last, -ops[last]["lag"])
+            last = i
+        for w, wr in accesses(o):
+            w = wide(w)
+            l = log.setdefault(w[0], [])
+            if wr:
+                l[:] = [e for e in l if e[2] == i or not holds(w, e[0])]
+            l.append((w, wr, i))
+    after = [[] for _ in ops]
+    for i in range(n):
+        for j in before[i]:
+            after[j].append(i)
+    way = [0.0] * n
+    for i in reversed(range(n)):
+        o = ops[i]
+        way[i] = o["cost"] + o["lag"] + max([way[k] + before[k][i] + OWN for k in after[i]], default=0.0)
+    missing = [len(b) for b in before]
+    ready = [i for i in range(n) if missing[i] == 0]
+    busy = {}
+    start, end, queue = [0.0] * n, [0.0] * n, [""] * n
+    while ready:
+        i = max(ready, key=lambda k: (way[k], -k))
+        ready.remove(i)
+        o, best = ops[i], None
+        for q in o["qs"] or ["-"]:
+            t = 0.0
+            for j, gap in before[i].items():
+                wake = 0.0 if q == "-" else SYNC if queue[j] != q else OWN if q in "vs" else 0.0
+                t = max(t, end[j] + gap + wake)
+            if q != "-":
+                for s, e in busy.setdefault(q, []):
+                    if t + o["cost"] <= s + 1e-9:
+                        break
+                    t = max(t, e)
+            if best is None or t < best[0] - 1e-9:
+                best = (t, q)
+        start[i], queue[i] = best
+        end[i] = start[i] + o["cost"] + o["lag"]
+        if queue[i] != "-":
+            busy[queue[i]] = sorted(busy[queue[i]] + [(start[i], start[i] + o["cost"])])
+        for k in after[i]:
+            missing[k] -= 1
+            if missing[k] == 0:
+                ready.append(k)
+    return sorted(range(n), key=lambda i: (start[i], i)), queue
+
+
 def rank_program(g, core, T, topo):
     r = T.rank_of(core)
     if r is None:
         return
     queues = {"v": g.vector, "s": g.scalar, "p": g.tensor, "q": g, "y": g.sync}
-    total = {}
-    known = {k: {} for k in queues}
-    clocks = {}
-    log = {}
+    ops = []
 
     def ap(w):
         n, p0, p1, c0, c1, st = w
         return T[n][p0:p1, c0:c1] if st == 1 else T[n][p0:p1, c0:c1:st]
 
-    def wide(w):
-        if w[0] != "ps":
-            return w
-        return ("ps", 0, 128, w[3] // 512 * 512, (w[4] + 511) // 512 * 512, 1)
-
-    def await_(q, need):
-        for s, n in sorted(need.items()):
-            if known[q].get(s, 0) < n:
-                queues[q].wait_ge(T.sem[s], n)
-                for s2, n2 in clocks.get((s, n), {}).items():
-                    known[q][s2] = max(known[q].get(s2, 0), n2)
-                known[q][s] = n
-
-    def note(sem, n, q, reads, writes):
-        for w, wr in [(x, False) for x in reads] + [(x, True) for x in writes]:
-            w = wide(w)
-            l = log.setdefault(w[0], [])
-            if wr:
-                l[:] = [e for e in l if not holds(w, e[0])]
-            l.append((w, wr, sem, n, q))
-
-    def op(q, fn, reads, writes, sem=None, inc=1, local=True):
-        need = {}
-        for w, wr in [(x, False) for x in reads] + [(x, True) for x in writes]:
-            for e in log.get(w[0], []):
-                other = w[0] == "ps" and e[4] != q
-                if (wr or e[1] or other) and meet(wide(w), e[0]):
-                    need[e[2]] = max(need.get(e[2], 0), e[3])
-        await_(q, need)
-        sem = sem or q
-        ins = fn(queues[q])
-        if local:
-            ins.then_inc(T.sem[sem], inc)
-        total[sem] = total.get(sem, 0) + inc
-        clocks[(sem, total[sem])] = dict(known[q])
-        note(sem, total[sem], q, reads, writes)
+    def op(qs, fn, reads, writes, cost, sem=None, inc=1, local=True, lag=0.0):
+        ops.append({"qs": qs, "fn": fn, "rd": reads, "wr": writes, "cost": cost, "sem": sem, "inc": inc, "local": local, "lag": lag})
 
     def val(x):
         return ap(x) if isinstance(x, tuple) else x
+
+    def time(n, *sides):
+        if sides and all(SCRATCH[w[0]][2] == HALF for w in sides):
+            n = n / 2
+        return max(64, n) * CYCLE
 
     def act(o, i, func=AF.Copy, bias=None, scale=None, acc=None):
         kw = {}
         for k, x in (("bias", bias), ("scale", scale), ("accum_out", acc)):
             if x is not None:
                 kw[k] = val(x)
-        op("s", lambda e: e.activation(ap(o), ap(i), func, **kw), [i] + [x for x in (bias, scale) if isinstance(x, tuple)],
-           [o] + ([acc] if acc is not None else []))
+        op("s", lambda e, q: e.activation(ap(o), ap(i), func, **kw), [i] + [x for x in (bias, scale) if isinstance(x, tuple)],
+           [o] + ([acc] if acc is not None else []), time(width(i)) + (0.025 if acc is not None else 0.0))
 
     def ts(o, i, s1, op0, s2=None, op1=None):
         rd = [i] + [s for s in (s1, s2) if isinstance(s, tuple)]
         if op1 is None:
-            op("v", lambda e: e.tensor_scalar(ap(o), ap(i), val(s1), None, op0), rd, [o])
+            op("v", lambda e, q: e.tensor_scalar(ap(o), ap(i), val(s1), None, op0), rd, [o], time(width(i), o, i))
         else:
-            op("v", lambda e: e.tensor_scalar(ap(o), ap(i), val(s1), val(s2), op0, op1), rd, [o])
+            op("v", lambda e, q: e.tensor_scalar(ap(o), ap(i), val(s1), val(s2), op0, op1), rd, [o], time(width(i), o, i))
 
-    def copy(q, o, i, scale=None):
-        if q == "s":
-            act(o, i, scale=scale)
-        elif scale is None:
-            op("v", lambda e: e.tensor_copy(ap(o), ap(i)), [i], [o])
-        else:
-            ts(o, i, scale, MUL)
+    def copy(o, i, scale=None, qs="vs"):
+        def fn(e, q):
+            if q == "v":
+                return e.tensor_copy(ap(o), ap(i)) if scale is None else e.tensor_scalar(ap(o), ap(i), scale, None, MUL)
+            return e.activation(ap(o), ap(i), AF.Copy) if scale is None else e.activation(ap(o), ap(i), AF.Copy, scale=scale)
+        op(qs, fn, [i], [o], time(width(i)))
 
-    def total_v(o, i):
-        op("v", lambda e: e.tensor_reduce(ap(o), ap(i), AxisListType.X, ADD), [i], [o])
+    def spread(o, x):
+        z = view("Z32", 0, 32, o[1], o[2])
+
+        def fn(e, q):
+            if q == "v":
+                return e.tensor_scalar(ap(o), ap(z), ap(x), None, ADD)
+            return e.activation(ap(o), ap(z), AF.Identity, bias=ap(x))
+        op("vs", fn, [z, x], [o], time(32))
 
     junk = [0]
 
+    def waste(i):
+        junk[0] += width(i)
+        return view("J4", junk[0] - width(i), junk[0], i[1], i[2])
+
+    def sums(o, i):
+        j = waste(i)
+
+        def fn(e, q):
+            if q == "v":
+                return e.tensor_reduce(ap(o), ap(i), AxisListType.X, ADD)
+            return e.activation(ap(j), ap(i), AF.Copy, accum_out=ap(o))
+        op("vs", fn, [i], [o, j], time(width(i)) + 0.01)
+
+    def count(name, c0, i):
+        n, p0, p1, a, b, _ = i
+        m = (a + b) // 2
+        o, x, y = view(name, c0, c0 + m - a, p0, p1), view(n, a, m, p0, p1), view(n, m, b, p0, p1)
+        op("v", lambda e, q: e.tensor_tensor_scan(ap(o), ap(x), ap(y), 0.0, ADD, ADD), [x, y], [o], time(m - a, o, x))
+
     def signs(i, bias, acc, scale=1.0):
-        o = view("J4", junk[0], junk[0] + 128)
-        junk[0] += 128
-        act(o, i, AF.Sign, bias=bias, scale=scale, acc=acc)
+        act(waste(i), i, AF.Sign, bias=bias, scale=scale, acc=acc)
 
     def tt(o, a, b, o0):
-        op("v", lambda e: e.tensor_tensor(ap(o), ap(a), ap(b), o0), [a, b], [o])
+        op("v", lambda e, q: e.tensor_tensor(ap(o), ap(a), ap(b), o0), [a, b], [o], time(2 * width(a)))
 
     def fill(o, c):
-        op("v", lambda e: e.memset(ap(o), c), [], [o])
+        op("v", lambda e, q: e.memset(ap(o), c), [], [o], time(width(o), o))
 
     def turn(o, i):
-        op("v", lambda e: e.transpose(ap(o), ap(i)), [i], [o])
+        op("v", lambda e, q: e.transpose(ap(o), ap(i)), [i], [o], time(width(i)))
 
-    def swap(name, n, engines):
-        copy(engines[0], view(name, n, 2 * n, 64, 128), view(name, 0, n, 0, 64))
-        copy(engines[1], view(name, n, 2 * n, 0, 64), view(name, 0, n, 64, 128))
+    def swap(name, n):
+        copy(view(name, n, 2 * n, 64, 128), view(name, 0, n, 0, 64))
+        copy(view(name, n, 2 * n, 0, 64), view(name, 0, n, 64, 128))
         for a in range(4):
-            copy(engines[a % 2], quarter(name, a, 2 * n, 4 * n), quarter(name, a ^ 1, 0, 2 * n))
-
-    def cross(dst, src, n, quarters):
-        k = 0
-        for a in range(quarters):
-            for b in range(4):
-                copy("vs"[k % 2], quarter(dst, b, a * n, a * n + n), quarter(src, a, 0, n))
-                k += 1
+            copy(quarter(name, a, 2 * n, 4 * n), quarter(name, a ^ 1, 0, 2 * n))
 
     def quant(dst, c0, n, src, e0=0):
         o, s, i = view(dst, c0, c0 + n), view("s" + dst, c0, c0 + n), view(src, e0, e0 + 4 * n)
-        op("v", lambda e: e.quantize_mx(ap(o), ap(s), ap(i)), [i], [o, s])
+        op("v", lambda e, q: e.quantize_mx(ap(o), ap(s), ap(i)), [i], [o, s], 0.015 + 0.001 * n)
 
     def mm(bk, w, wc, x, xc, n):
         o = view("ps", 512 * bk, 512 * bk + n)
         a, sa, b, sb = view(w, wc, wc + 128), view("s" + w, wc, wc + 128), view(x, xc, xc + n), view("s" + x, xc, xc + n)
-        op("p", lambda e: e.matmul_mx(ap(o), ap(a), ap(sa), ap(b), ap(sb), True, True), [a, sa, b, sb], [o])
+        op("p", lambda e, q: e.matmul_mx(ap(o), ap(a), ap(sa), ap(b), ap(sb), True, True), [a, sa, b, sb], [o], 1.3 * CYCLE * (n + 16))
 
     def bank(i, n, p0=0, p1=128, c0=0):
         return view("ps", 512 * i + c0, 512 * i + c0 + n, p0, p1)
 
-    def load(q, name, dst, n, sem):
+    def load(q, name, dst, n, sem, more=0.0):
         o = view(dst, 0, n)
-        op(q, lambda e: e.dma_start(ap(o), T[name][:, 0:n]), [], [o], sem, 16)
+        op(q, lambda e, q: e.dma_start(ap(o), T[name][:, 0:n]), [], [o], 0.06, sem, 16, lag=LOCAL + more)
+
+    def store(fn, i, sem):
+        op("ys", lambda e, q: fn(e), [i], [], 0.06, sem, 16, lag=LOCAL)
 
     def move(q, dst, d0, src, s0, n, s1, s2):
         o, i, os, is_ = view(dst, d0, d0 + n), view(src, s0, s0 + n), view("s" + dst, d0, d0 + n), view("s" + src, s0, s0 + n)
-        op(q, lambda e: e.dma_start(ap(o).bitcast(dt.uint8), ap(i).bitcast(dt.uint8)), [i], [o], s1, 16)
-        op(q, lambda e: e.dma_start(ap(os), ap(is_)), [is_], [os], s2, 16)
+        op(q, lambda e, q: e.dma_start(ap(o).bitcast(dt.uint8), ap(i).bitcast(dt.uint8)), [i], [o], 0.06, s1, 16, lag=LOCAL)
+        op(q, lambda e, q: e.dma_start(ap(os), ap(is_)), [is_], [os], 0.06, s2, 16, lag=LOCAL)
 
     others = [d for d in range(N) if d != r]
     where = [topo.addr(T.cores[d], core) for d in others]
@@ -212,7 +274,7 @@ def rank_program(g, core, T, topo):
             dsts.append(T[land][:, k * j:k * j + k])
         tr = RemoteDMATransfer(dst_ids=[DstId(rid=int(a), pnc=int(b)) for a, b in where], dma_engine_mask=mask,
                                remote_sem=T.sem[sem], srcs=[ap(src)], dsts=dsts, alu_op=0)
-        op("q", lambda e: e.remote_dma_fused([tr], local_sem=T.sem.left), [src], [], "left", lanes, False)
+        op("q", lambda e, q: e.remote_dma_fused([tr], local_sem=T.sem.left), [src], [], 1.0, "left", lanes, False, FLY)
 
     def to_one(d, d0, s0, n):
         rid, pid = topo.addr(T.cores[d], core)
@@ -220,31 +282,28 @@ def rank_program(g, core, T, topo):
         ln = bin(m).count("1")
         c, s = view("SRC", s0, s0 + n), view("sSRC", s0, s0 + n)
         oc, os = T.SRC[:, d0:d0 + n].bitcast(dt.uint8), T.sSRC[:, d0:d0 + n]
-        op("q", lambda e: e.remote_dma(oc, ap(c).bitcast(dt.uint8), T.sem.halo, T.sem.left, pid, rid, m), [c], [], "left", ln, False)
-        op("q", lambda e: e.remote_dma(os, ap(s), T.sem.halo, T.sem.left, pid, rid, m), [s], [], "left", ln, False)
+        op("q", lambda e, q: e.remote_dma(oc, ap(c).bitcast(dt.uint8), T.sem.halo, T.sem.left, pid, rid, m), [c], [], 0.7, "left", ln, False, FLY)
+        op("q", lambda e, q: e.remote_dma(os, ap(s), T.sem.halo, T.sem.left, pid, rid, m), [s], [], 0.7, "left", ln, False, FLY)
 
     def arrive(sem, n, writes):
-        total[sem] = n
-        note(sem, n, None, [], writes)
+        ops.append({"qs": "", "fn": None, "rd": [], "wr": writes, "cost": 0.0, "sem": sem, "inc": n, "local": False, "lag": 0.0,
+                    "behind": max(k for k, o in enumerate(ops) if o["sem"] == "left")})
 
     load("s", "u", "UC", 4, "du")
-    load("y", "x", "XT", 4 * P, "dx")
-    load("y", "a", "AT", 2048, "da")
-    load("s", "b", "BT", 2048, "db")
-    load("y", "w", "WT", 512, "dw")
-    op("q", lambda e: e.iota(T.PI[:], [[0, 1]], 0, 1), [], [view("PI")])
-    op("q", lambda e: e.iota(T.FI[:], [[1, 96]], 0, 0, allow_small_or_imprecise_dtypes=True), [], [view("FI")])
+    load("y", "x", "XT", 4 * P, "dx", 0.5)
+    load("y", "a", "AT", 2048, "da", 2.0)
+    load("s", "b", "BT", 2048, "db", 2.0)
+    load("y", "w", "WT", 512, "dw", 2.0)
+    op("q", lambda e, q: e.iota(T.PI[:], [[0, 1]], 0, 1), [], [view("PI")], 0.16)
+    op("q", lambda e, q: e.iota(T.FI[:], [[1, 96]], 0, 0, allow_small_or_imprecise_dtypes=True), [], [view("FI")], 0.37)
     fill(view("Z32"), 0.0)
     fill(view("ZB"), 0.0)
     fill(view("XT", 4 * P, 512), 0.0)
-    fill(view("GM"), 1.0)
-    fill(view("GM", 0, 224, step=32), 0.0)
-    fill(view("Z1"), 0.0)
-    op("v", lambda e: e.tensor_scalar(T.PM[:, 0:1], T.PI[:], 31, None, AluOpType.bitwise_and), [view("PI")], [view("PM", 0, 1)])
-    op("v", lambda e: e.tensor_scalar(T.PM[:, 1:2], T.PI[:], 15, None, AluOpType.bitwise_and), [view("PI")], [view("PM", 1, 2)])
-    copy("v", view("PF"), view("PI"))
-    copy("v", view("X32"), view("PM", 0, 1))
-    copy("v", view("X16"), view("PM", 1, 2))
+    op("v", lambda e, q: e.tensor_scalar(T.PM[:, 0:1], T.PI[:], 31, None, AluOpType.bitwise_and), [view("PI")], [view("PM", 0, 1)], time(1))
+    op("v", lambda e, q: e.tensor_scalar(T.PM[:, 1:2], T.PI[:], 15, None, AluOpType.bitwise_and), [view("PI")], [view("PM", 1, 2)], time(1))
+    copy(view("PF"), view("PI"), qs="v")
+    copy(view("X32"), view("PM", 0, 1), qs="v")
+    copy(view("X16"), view("PM", 1, 2), qs="v")
     tt(view("PA"), view("PF"), view("X32"), SUB)
     tt(view("XA"), view("X32"), view("PA"), SUB)
     tt(view("PB"), view("PA"), view("X16"), ADD)
@@ -253,6 +312,7 @@ def rank_program(g, core, T, topo):
         for buf, c, v in (("KAP", 0, 4.0 * P * r + sigma[a]), ("FC", 0, 2.0 - 0.5 * sigma[a] + 127.0), ("WC", 0, 2.0 * P * alpha[a]),
                           ("WC", 1, 2.0 * P * beta[a]), ("WC", 2, float(sigma[a])), ("WC", 3, -2.0 * P * beta[a])):
             act(quarter(buf, a, c, c + 1), quarter("Z32", a, 0, 1), bias=v)
+        act(quarter("THR", a), quarter("Z32", a), bias=-BIG * (K - 0.5 if a < 3 else 1000.0))
     for t in range(4):
         ts(view("UT", t, 512, step=4), view("ZB"), view("UC", t, t + 1), ADD)
     quant("QU", 0, 128, "UT")
@@ -260,8 +320,8 @@ def rank_program(g, core, T, topo):
 
     mm(0, "SRC", 0, "QU", 0, 128)
     mm(1, "QU", 0, "SRC", 0, 128)
-    copy("s", view("X1S"), bank(0, 1))
-    copy("v", view("SROW"), bank(1, 96))
+    copy(view("X1S"), bank(0, 1))
+    copy(view("SROW"), bank(1, 96))
     to_all(view("X1S"), "X1L", 1, "x1")
     arrive("x1", 7 * lanes, [view("X1L")])
     if r < N - 1:
@@ -284,7 +344,7 @@ def rank_program(g, core, T, topo):
 
     turn(view("TS"), view("SROW"))
     for a in range(4):
-        act(quarter("SQ", a), quarter("SROW", a, 32 * (a % 3), 32 * (a % 3) + 32))
+        copy(quarter("SQ", a), quarter("SROW", a, 32 * (a % 3), 32 * (a % 3) + 32))
     quant("QA", 0, 512, "AT")
     for i in range(4):
         mm(i, "QA", 128 * i, "SRC", 0, 128)
@@ -292,7 +352,7 @@ def rank_program(g, core, T, topo):
     for i in range(4):
         mm(4 + i, "QB", 128 * i, "SRC", 0, 128)
     for i in range(8):
-        copy("s", view("KT", i % 4 + 384 * (i // 4), 384 + 384 * (i // 4), step=4), bank(i, 96), 0.0625)
+        copy(view("KT", i % 4 + 384 * (i // 4), 384 + 384 * (i // 4), step=4), bank(i, 96), 0.0625)
     for b in range(3):
         ts(view("XB", b, b + 1), view("XA"), 32.0 * b, ADD)
     for b in range(3):
@@ -301,24 +361,24 @@ def rank_program(g, core, T, topo):
         ts(view("OE", 32 * b, 32 * b + 32), view("SQ"), s, EQ)
         ts(view("CM", o + 224, o + 256), view("SQ"), s, GT)
         tt(view("CM", o + 256, o + 288), view("OE", 32 * b, 32 * b + 32), view("TRI", 32 * b, 32 * b + 32), MUL)
-    copy("v", view("JC"), view("X32"))
+    copy(view("JC"), view("X32"))
     ts(quarter("JC", 2), quarter("X32", 2), 32.0, ADD)
     ts(view("KV"), view("FI"), 4.0, MUL, view("KAP"), ADD)
-    fill(quarter("VR", 3), HUGE)
-    copy("v", quarter("VR", 2), quarter("SROW", 2))
+    fill(quarter("VR", 3), -HUGE)
+    copy(quarter("VR", 2), quarter("SROW", 2))
     quant("SRC", P, 2 * P, "KT")
     mm(0, "QU", 0, "SRC", P, 2 * P)
-    copy("v", quarter("VR", 0), bank(0, 96, 0, 32))
-    copy("v", quarter("VR", 1), bank(0, 96, 32, 64, 96))
+    copy(quarter("VR", 0), bank(0, 96, 0, 32))
+    copy(quarter("VR", 1), bank(0, 96, 32, 64, 96))
     for i in range(4):
         mm(1 + i, "QA", 128 * i, "SRC", P, 2 * P)
     for i in range(4):
         mm((5 + i) % 8, "QB", 128 * i, "SRC", P, 2 * P)
     for i in range(4):
-        copy("s", view("GO", i, 768, step=4), bank(1 + i, 192), 0.0625)
+        copy(view("GO", i, 768, step=4), bank(1 + i, 192), 0.0625)
 
-    copy("v", view("Z1", 0, 224, step=32), view("X1L"))
-    op("v", lambda e: e.tensor_tensor_scan(T.EX1[:], T.GM[:], T.Z1[:], 0.0, MUL, ADD), [view("GM"), view("Z1")], [view("EX1")])
+    for j in range(N - 1):
+        spread(view("EX1", 32 * j, 32 * j + 32), view("X1L", j, j + 1))
     turn(view("R1"), view("EX1"))
     for b in range(3):
         s, o = view("TS", 32 * b, 32 * b + 1), 288 * b
@@ -326,44 +386,43 @@ def rank_program(g, core, T, topo):
             ts(view("CM", o, o + 32 * r), view("R1", 0, 32 * r), s, GE)
         if r < N - 1:
             ts(view("CM", o + 32 * r, o + 224), view("R1", 32 * r, 224), s, GT)
-        if b < 2:
-            act(view("J1", o, o + 288), view("CM", o, o + 288), acc=view("CN", b, b + 1))
-        else:
-            total_v(view("CN", b, b + 1), view("CM", o, o + 288))
-    copy("v", quarter("CA", 0, 0, 3), quarter("CN", 1))
-    copy("s", quarter("CA", 0, 3, 6), quarter("CN", 2))
-    tt(quarter("U2", 0), quarter("CA", 0, 0, 3), quarter("CA", 0, 3, 6), ADD)
+        count("CN", 144 * b, view("CM", o, o + 288))
+    copy(quarter("CA", 0, 0, 3), quarter("CN", 1, 143, 432, 144))
+    copy(quarter("CA", 0, 3, 6), quarter("CN", 2, 143, 432, 144))
     for b in range(3):
-        ts(quarter("EX3", 0, 32 * b, 32 * b + 32), quarter("Z32", 0), quarter("CN", 0, b, b + 1), ADD, quarter("U2", 0, b, b + 1), ADD)
+        spread(quarter("E0", 0, 32 * b, 32 * b + 32), quarter("CN", 0, 144 * b + 143, 144 * b + 144))
+        ts(quarter("EX3", 0, 32 * b, 32 * b + 32), quarter("E0", 0, 32 * b, 32 * b + 32), quarter("CA", 0, b, b + 1), ADD,
+           quarter("CA", 0, 3 + b, 4 + b), ADD)
     turn(quarter("PR", 0), quarter("EX3", 0))
     for a in (1, 2, 3):
-        copy("vsv"[a - 1], quarter("PR", a), quarter("PR", 0))
+        copy(quarter("PR", a), quarter("PR", 0))
     ts(view("OH"), view("PR"), view("JC"), EQ)
     tt(view("M2"), view("OH"), view("KV"), MUL)
-    act(view("J2"), view("M2"), acc=view("XS", 1, 2))
+    sums(view("XS", 1, 2), view("M2"))
     tt(view("M1"), view("OH"), view("VR"), MUL)
-    total_v(view("XS", 0, 1), view("M1"))
+    sums(view("XS", 0, 1), view("M1"))
     to_all(view("XS"), "X2L", 2, "x2")
     arrive("x2", 7 * lanes, [view("X2L")])
 
     for i in range(4):
         mm(1 + i, "QA", 128 * i, "SRC", H0 - 56, 128)
     for i in range(4):
-        copy("vs"[i % 2], view("GO", 768 + i, 1536, step=4), bank((5 + i) % 8, 192), 0.0625)
+        copy(view("GO", 768 + i, 1536, step=4), bank((5 + i) % 8, 192), 0.0625)
     for i in range(4):
         mm((5 + i) % 8, "QB", 128 * i, "SRC", H0 - 56, 128)
     fill(view("HK", 4 * HN, 4 * P), 0.0)
     fill(view("HG", 4 * 168, 4 * 192), 0.0)
     for i in range(8):
         e0 = 4 * P * (i // 4)
-        copy("vs"[i % 2], view("HK", e0 + i % 4, e0 + 4 * HN, step=4), bank((1 + i) % 8, HN, c0=56), 0.0625)
+        copy(view("HK", e0 + i % 4, e0 + 4 * HN, step=4), bank((1 + i) % 8, HN, c0=56), 0.0625)
     quant("SRC", H0 + P, P + HN, "HK")
     for i in range(8):
         mm((1 + i) % 8, "QA" if i < 4 else "QB", 128 * (i % 4), "SRC", H0 + P, P + HN)
-    quant("SRC", 3 * P, 4 * P, "GO")
+    for i in range(3):
+        quant("SRC", 3 * P + 128 * i, 128, "GO", 512 * i)
     for h in range(2):
         ts(view("PC", h, h + 1), view("PB"), 16.0 * h, ADD, E - 1.0, MIN)
-    swap("WC", 4, "ss")
+    swap("WC", 4)
     act(view("P2"), view("PC"), bias=2.0 * E * r, scale=2.0)
     act(view("PN"), view("PC"), bias=2.0 * E * r + 2.0, scale=2.0)
     act(view("NN"), view("PC", 1, 2), bias=-2.0 * E * r - 2.0, scale=-2.0)
@@ -373,33 +432,30 @@ def rank_program(g, core, T, topo):
     act(view("H2"), view("PF"), bias=2.0 * E * r, scale=2.0)
     act(view("NH"), view("PF"), bias=-2.0 * E * r - 1.0, scale=-2.0)
     act(view("WH", 128, 129), view("PF"), bias=4.0 * E * r - 256.0, scale=4.0)
-    fill(view("W", 258, 528, step=264), 0.0)
-    fill(view("W", 259, 528, step=264), 0.0)
+    if r == 0:
+        fill(view("W", 258, 528, step=264), 0.0)
+    if r == N - 1:
+        fill(view("W", 259, 528, step=264), 0.0)
     quant("QW", 0, 128, "WT")
     for i in range(8):
         e0 = 4 * 192 * (i // 4)
-        copy("vs"[i % 2], view("HG", e0 + i % 4, e0 + 4 * 168, step=4), bank((1 + i) % 8, 168), 0.0625)
-    quant("SRC", H0 + 3 * P, 360, "HG")
+        copy(view("HG", e0 + i % 4, e0 + 4 * 168, step=4), bank((1 + i) % 8, 168), 0.0625)
+    for i in range(2):
+        quant("SRC", H0 + 3 * P + 180 * i, 180, "HG", 720 * i)
 
-    for k in range(2):
-        total_v(view("SC", k, k + 1), view("X2L", k, 14, step=2))
-    for k in (1, 0):
-        ts(view("EX2", 32 * k, 32 * k + 32), view("Z32"), view("SC", k, k + 1), ADD, view("XS", k, k + 1), ADD)
-    turn(view("R2"), view("EX2"))
-    cross("D", "R2", 64, 3)
     sc, mc = view("EX2", 0, 1), view("EX2", 32, 33)
-    for a in range(3):
-        ts(view("EQ", 32 * a, 32 * a + 32), view("D", 64 * a, 64 * a + 32), sc, EQ)
-        act(view("KS", 32 * a, 32 * a + 32), view("D", 64 * a + 32, 64 * a + 64), AF.Sign, bias=mc, scale=-1.0)
-    act(view("KL"), view("KS"), AF.Relu)
-    for a in range(3):
-        ts(view("GE", 32 * a, 32 * a + 32), view("D", 64 * a, 64 * a + 32), sc, GT)
-    tt(view("GE", 96, 192), view("EQ"), view("KL"), MUL)
-    total_v(view("P1"), view("GE"))
-    ts(view("PEN"), view("P1"), float(K), GE, BIG, MUL)
-    ts(view("EXM"), view("Z32"), view("PEN"), ADD, mc, ADD)
+    for k, row in ((0, "DS"), (1, "DN")):
+        sums(view("SC", k, k + 1), view("X2L", k, 14, step=2))
+        ts(view("EX2", 32 * k, 32 * k + 32), view("Z32"), view("SC", k, k + 1), ADD, view("XS", k, k + 1), ADD)
+        turn(view(row, 0, 32), view("EX2", 32 * k, 32 * k + 32))
+        swap(row, 32)
+    act(view("SG"), view("DS"), AF.Sign, bias=sc, scale=-1.0)
+    ts(view("LO"), view("DN"), mc, GE, -0.5, MUL)
+    tt(view("BF"), view("SG"), view("LO"), LE)
+    act(waste(view("BF")), view("BF"), scale=BIG, acc=view("P1"))
+    ts(view("EXM"), view("THR"), view("P1"), ADD, mc, MAX)
     turn(view("MR", 0, 32), view("EXM"))
-    swap("MR", 32, "vs")
+    swap("MR", 32)
     signs(view("MR"), view("EXM", 0, 1), view("RK"), -1.0)
     ts(view("F0"), view("EXM", 0, 1), 0.5, MUL, view("FC"), ADD)
     if r > 0:
@@ -408,7 +464,7 @@ def rank_program(g, core, T, topo):
         signs(view("MR"), 4.0 * P * (r + 1) - 0.5, view("SB", 1, 2), -1.0)
     ts(view("EXF"), view("Z32"), view("RK"), ADD, view("F0"), ADD)
     turn(view("FR", 0, 32), view("EXF"))
-    swap("FR", 32, "vs")
+    swap("FR", 32)
 
     for h in range(2):
         signs(view("FR"), view("NS", h, h + 1), view("W", 264 * h + 257, 264 * h + 258))
@@ -427,25 +483,64 @@ def rank_program(g, core, T, topo):
             if h == 0:
                 ts(view("W", c + 128, c + 160), f, view("PN", h, h + 1), EQ, view("WC", 4 * k + 1, 4 * k + 2), MUL)
     for h in range(2):
-        total_v(view("OF", h, h + 1), view("W", 264 * h, 264 * h + 260))
-    cross("OTF", "OF", 2, 4)
+        count("OF", 130 * h, view("W", 264 * h, 264 * h + 260))
+    for a in range(4):
+        for b in range(4):
+            copy(quarter("OTF", b, 2 * a, 2 * a + 2), quarter("OF", a, 129, 260, 130))
     ts(view("OT"), view("OTF"), 0.5, MUL)
-    op("v", lambda e: e.tensor_copy(T.RUN[:, 0:128].bitcast(dt.uint32), T.SRC[:, 0:ALL].bitcast(dt.uint32).indirect(T.OT[:, 0:8])),
-       [view("SRC"), view("OT")], [view("RUN")])
-    op("s", lambda e: e.activation(T.sRUN[:, 0:128], T.sSRC[:, 0:ALL].indirect(T.OT[:, 0:8]), AF.Copy),
-       [view("sSRC"), view("OT")], [view("sRUN")])
+    op("v", lambda e, q: e.tensor_copy(T.RUN[:, 0:128].bitcast(dt.uint32), T.SRC[:, 0:ALL].bitcast(dt.uint32).indirect(T.OT[:, 0:8])),
+       [view("SRC"), view("OT")], [view("RUN")], 0.26)
+    op("s", lambda e, q: e.activation(T.sRUN[:, 0:128], T.sSRC[:, 0:ALL].indirect(T.OT[:, 0:8]), AF.Copy),
+       [view("sSRC"), view("OT")], [view("sRUN")], 0.28)
 
     mm(0, "QW", 0, "RUN", 0, 128)
+    copy(view("YT"), bank(0, E))
+    store(lambda e: e.dma_start(T.y[:, 0:E], T.YT[:]), view("YT"), "o5")
+    store(lambda e: e.dma_start(T.oc[:, 0:4 * E], T.RUN[:, 0:E].bitcast(dt.uint8)), view("RUN", 0, E), "o0")
+    for k in range(4):
+        store(lambda e, k=k: e.dma_start(T.osc[4 * k:4 * k + 4, 0:E], T.sRUN[32 * k:32 * k + 4, 0:E]), view("sRUN", 0, E, 32 * k, 32 * k + 4), "o%d" % (1 + k))
     for k in (129, 130):
         signs(view("FR"), view("NH"), view("WH", k, k + 1))
-    copy("s", view("YT"), bank(0, E))
-    op("s", lambda e: e.dma_start(T.y[:, 0:E], T.YT[:]), [view("YT")], [], "o5", 16)
-    op("y", lambda e: e.dma_start(T.oc[:, 0:4 * E], T.RUN[:, 0:E].bitcast(dt.uint8)), [view("RUN", 0, E)], [], "o0", 16)
-    for k in range(4):
-        op("yyss"[k], lambda e: e.dma_start(T.osc[4 * k:4 * k + 4, 0:E], T.sRUN[32 * k:32 * k + 4, 0:E]),
-           [view("sRUN", 0, E, 32 * k, 32 * k + 4)], [], "o%d" % (1 + k), 16)
     for k in range(4):
         ts(view("WH", 32 * k, 32 * k + 32), view("FR", 32 * k, 32 * k + 32), view("H2"), EQ, view("WC", 4 * k + 2, 4 * k + 3), MUL)
-    total_v(view("HB"), view("WH", 0, 131))
-    op("y", lambda e: e.dma_start(T.hs[0:1, 0:E], T.HB[0:E, 0:1]), [view("HB", 0, 1, 0, E)], [], "o6", 16)
+    sums(view("HB"), view("WH", 0, 131))
+    store(lambda e: e.dma_start(T.hs[0:1, 0:E], T.HB[0:E, 0:1]), view("HB", 0, 1, 0, E), "o6")
+
+    order, queue = place(ops)
+    total = {}
+    known = {k: {} for k in queues}
+    clocks = {}
+    log = {}
+
+    def await_(q, need):
+        for s, n in sorted(need.items()):
+            if known[q].get(s, 0) < n:
+                queues[q].wait_ge(T.sem[s], n)
+                for s2, n2 in clocks.get((s, n), {}).items():
+                    known[q][s2] = max(known[q].get(s2, 0), n2)
+                known[q][s] = n
+
+    for i in order:
+        o, q = ops[i], queue[i]
+        sem = o["sem"] or q
+        if o["fn"] is not None:
+            need = {}
+            for w, wr in accesses(o):
+                for v, vr, s, n, q2 in log.get(w[0], []):
+                    if (wr or vr or (w[0] == "ps" and q2 != q)) and meet(wide(w), v):
+                        need[s] = max(need.get(s, 0), n)
+            await_(q, need)
+            ins = o["fn"](queues[q], q)
+            if o["local"]:
+                ins.then_inc(T.sem[sem], o["inc"])
+            total[sem] = total.get(sem, 0) + o["inc"]
+            clocks[(sem, total[sem])] = dict(known[q])
+        else:
+            total[sem] = o["inc"]
+        for w, wr in accesses(o):
+            w = wide(w)
+            l = log.setdefault(w[0], [])
+            if wr:
+                l[:] = [e for e in l if not holds(w, e[0])]
+            l.append((w, wr, sem, total[sem], q))
     await_("y", total)

@@ -3,14 +3,43 @@ from concourse.mybir import dt, AluOpType, AxisListType, ActivationFunctionType
 
 N, P, K = 8, 96, 32
 E = P + 2 * K // N
-H0 = 7 * P
+AA, AB, BA, BB = 6, 7, 11, 12
+H0 = 3 * P
 HN = 72
-ALL = 14 * P - 24
-BIG = 1048576.0
+ALL = H0 + BB * P + HN
+UNIT = 2.0 ** -20
 HUGE = 1.0e29
 CODE = "float8_e4m3fn_x4"
 HALF = "bfloat16"
 CYCLE, SYNC, OWN, FLY, LOCAL = 0.0009, 0.16, 0.14, 1.6, 2.0
+ORDER = """
+load.u:s XT.0.384:v load.x:y Z32.0.0:v U0.0.8:v load.a:y KAP.3.0:s PI.0.0:q PM.0.1:v KAP.0.0:s VR.3.0:v THR.2.0:s ZB.0.0:v
+PF.0.0:v PM.0.0:v X16.0.0:v WC.1.2:s load.b:s X32.0.0:v PA.0.0:v QV.0.0:v load.w:y KAP.1.0:s WC.1.0:s SRC.0.0:v WC.1.1:s
+HK.0.288:v FI.0.0:q UT.0.3:v UT.0.1:v WC.2.3:s WC.3.2:s JC.0.0:s ps.0.0:p X1S.0.0:s KAP.2.0:s UT.0.0:v UT.0.2:v XA.0.0:v
+WC.0.0:s XB.0.0:v QU.0.0:v XB.0.2:v PB.0.0:v H2.0.0:s X2L.0.2:v ps.0.512:p XB.0.1:v SROW.0.0:s KV.0.0:v send.x1:q PC.0.0:v
+FC.1.0:s WC.1.3:s WC.2.2:s SQ.0.0:s PC.0.1:v WC.3.1:s TS.0.0:v THR.0.0:s WH.0.128:s WC.3.3:s JC.2.0:v codes.1:q WC.0.2:s
+SQ.2.0:s scales.1:q TRI.0.32:v QA.0.0:v QB.0.0:v WC.0.1:s SQ.3.0:v WC.3.0:s SQ.1.0:s ps.0.1024:p WC.2.1:s KT.0.2:s ps.0.1536:p
+OE.0.32:v OE.0.64:v ps.0.0.2:p VR.2.0:s ps.0.3584:p ps.0.3072:p FC.2.0:s KT.0.3:s WC.0.3:s TRI.0.64:v FC.3.0:s CM.0.512:v
+W.0.256:s codes.0:q OE.0.0:v CM.0.544:v TRI.0.0:v KT.0.0:v come.x1:- WC.2.4:s KT.0.387:s CM.0.800:v CM.0.224:v ps.0.2560:p
+CM.0.832:v CM.0.256:v EX1.0.192:v NS.0.0:s EX1.0.64:s ps.0.2048:p EX1.0.32:v EX1.0.96:s KT.0.386:s P2.0.0:s EX1.0.160:v
+ps.0.512.2:p FC.0.0:s KT.0.385:s EX1.0.0:v KT.0.384:s EX1.0.128:v KT.0.1:s R1.0.0:v WC.2.8:s CN.0.288:v GE.0:v GE.1:v
+scales.0:q SRC.0.96:v TG.0.0:s TA.1:s TA.0:s GT.0:v W.0.260:s WC.2.0:s GT.1:v NH.0.0:s CN.0.0:v WC.0.4:s CN.0.144:v E0.0.0:s
+CN.0.431:v CA.0.0:v CA.1.3:v CA.0.3:v ps.0.0.3:p CA.1.0:v E0.0.32:s PN.0.0:s WC.3.8:s THR.1.0:s E0.0.64:v VR.0.0:s EX3.0.0:v
+VR.1.0:s EX3.0.64:v EX3.0.32:v PR.2.0:v PR.0.0:v OH.0.0:v come.halo:- THR.3.0:s M2.0.0:v M1.0.0:v ps.0.2048.2:p ps.0.512.3:p
+XS.0.0:v ps.0.1536.2:p XS.0.1:s HK.0.2:v ps.0.3584.2:p WC.0.8:v HK.0.0:s X2L.0.0:s HK.0.386:s HK.0.3:v ps.0.1024.2:p
+ps.0.3072.2:p ps.0.2560.2:p GO.0.2:s WC.1.8:s NN.0.0:s ps.0.0.4:p send.x2:q HK.0.1:v GO.0.0:s HK.0.385:s GO.0.1:v GO.0.3:s
+QW.0.0:v HK.0.384:s GO.0.769:s GO.0.770:v SRC.0.576:v come.x2:- HK.0.387:v SRC.0.384:v SC.0.0:s SC.0.1:s GO.0.771:v EX2.0.32:v
+EX2.2.32:s EX2.0.0:s EX2.2.96:s EX2.0.96:v EX2.0.64:s DS.0.0:v GO.0.768:s ps.0.1536.3:p DS.1.64:s ps.0.3072.3:p DS.3.64:s
+DN.0.0:v ps.0.2048.3:p DS.0.64:v DN.0.64:s ps.0.1024.3:p DN.3.64:s DS.2.64:v SG.0.0:s DN.1.64:v DN.2.64:v SRC.0.1056:v LO.0.0:v
+ps.0.512.4:p HG.0.2:s HG.0.3:s HG.0.1:s BF.0.0:v P1.0.0:v HG.0.673:s HG.0.0:s EXM.0.0:v MR.0.0:v ps.0.2560.3:p MR.2.32:v
+HG.0.672:s MR.0.32:v F0.0.0:v MR.3.64:v MR.1.64:v F32.0.0:v MR.2.64:s ps.0.3584.3:p MR.0.64:s ps.0.0.5:p HG.0.674:s sg.RK.0:s
+EXF.2.32:s EXF.0.32:s SRC.0.864:v HG.0.675:v EXF.0.0:s SRC.0.1344:v FR.0.0:v FR.2.64:v FR.0.64:v sg.SB.1:s sg.SB.0:s FR.3.64:s
+FR.1.64:s W.0.32:v high:v low:v W.0.0:v W.0.264:v AB.0.0:s W.0.360:v sg.W.257:s W.0.392:s W.0.192:v W.0.96:v W.0.160:v
+W.0.224:v W.0.64:v W.0.128:v W.0.328:v sg.W.521:s W.0.488:s W.0.424:s W.0.296:v OF.0.0:v W.0.456:s OF.0.130:v WH.0.0:v
+OTF.2.6:v OTF.0.0:s OTF.2.0:v OTF.2.4:s OTF.0.2:v OTF.0.6:s OTF.1.4:v OTF.1.6:s OTF.2.2:s OTF.3.0:s OTF.0.4:v OTF.1.2:v
+OTF.3.4:v OTF.1.0:s OTF.3.2:v OTF.3.6:v OT.0.0:v sg.WH.129:s sRUN.0.0:s sg.WH.130:s RUN.0.0:v WH.0.64:v WH.0.96:v WH.0.32:v
+store.o2:y ps.0.0.6:p store.o4:s store.o3:y store.o1:y HB.0.0:s YT.0.0:s store.o5:s store.o0:y store.o6:y
+"""
 
 
 def _sb(n, d="float32"):
@@ -18,13 +47,13 @@ def _sb(n, d="float32"):
 
 
 SCRATCH = {
-    "XT": _sb(512, HALF), "UC": _sb(4, HALF), "UT": _sb(512, HALF), "ZB": _sb(128, HALF),
+    "XT": _sb(512, HALF), "U0": _sb(512, HALF), "UT": _sb(512, HALF), "ZB": _sb(128, HALF),
     "AT": _sb(2048, HALF), "BT": _sb(2048, HALF), "WT": _sb(512, HALF),
-    "QU": _sb(128, CODE), "sQU": _sb(128, "uint8"),
+    "QU": _sb(128, CODE), "sQU": _sb(128, "uint8"), "QV": _sb(128, CODE), "sQV": _sb(128, "uint8"),
     "QA": _sb(512, CODE), "sQA": _sb(512, "uint8"), "QB": _sb(512, CODE), "sQB": _sb(512, "uint8"),
     "QW": _sb(128, CODE), "sQW": _sb(128, "uint8"),
     "SRC": _sb(ALL, CODE), "sSRC": _sb(ALL, "uint8"),
-    "KT": _sb(768, HALF), "GO": _sb(1536, HALF), "HK": _sb(672, HALF), "HG": _sb(1440, HALF),
+    "KT": _sb(768, HALF), "GO": _sb(1536, HALF), "HK": _sb(672, HALF), "HG": _sb(1344, HALF),
     "RUN": _sb(128, CODE), "sRUN": _sb(128, "uint8"), "YT": _sb(E),
     "ps": ("psum", [128, 4096], "float32"),
     "Z32": _sb(32), "PI": _sb(1, "int32"), "PM": _sb(2, "int32"), "PF": _sb(1), "X32": _sb(1), "X16": _sb(1),
@@ -32,16 +61,16 @@ SCRATCH = {
     "PA": _sb(1), "PB": _sb(1), "PC": _sb(2), "P2": _sb(2), "PN": _sb(2), "NN": _sb(1), "NS": _sb(2), "H2": _sb(1), "NH": _sb(1),
     "WC": _sb(16), "THR": _sb(32),
     "X1S": _sb(1), "X1L": _sb(7), "SROW": _sb(96), "SQ": _sb(32), "TS": _sb(96), "OE": _sb(96),
-    "EX1": _sb(224), "R1": _sb(224), "CM": _sb(864, HALF), "CN": _sb(432, HALF), "CA": _sb(6),
+    "EX1": _sb(224), "R1": _sb(224), "CM": _sb(864, HALF), "CN": _sb(432, HALF), "CA": _sb(6), "TG": _sb(224, HALF), "TA": _sb(2),
     "E0": _sb(96), "EX3": _sb(96), "PR": _sb(96), "OH": _sb(96), "M1": _sb(96), "M2": _sb(96),
-    "XS": _sb(2), "X2L": _sb(14), "SC": _sb(2), "EX2": _sb(64), "DS": _sb(128), "DN": _sb(128), "SG": _sb(128, HALF), "LO": _sb(128, HALF),
-    "BF": _sb(128), "P1": _sb(1), "EXM": _sb(32), "MR": _sb(128),
-    "F0": _sb(1), "RK": _sb(1), "SB": _sb(2), "EXF": _sb(32), "FR": _sb(128), "J4": _sb(2048),
+    "XS": _sb(2), "X2L": _sb(20), "SC": _sb(2), "EX2": _sb(128), "DS": _sb(128), "DN": _sb(128), "SG": _sb(128, HALF), "LO": _sb(128, HALF),
+    "BF": _sb(128, HALF), "P1": _sb(64), "EXM": _sb(32), "MR": _sb(128),
+    "F0": _sb(1), "F32": _sb(32), "RK": _sb(1), "SB": _sb(2), "EXF": _sb(64), "FR": _sb(128), "J4": _sb(2304),
     "W": _sb(528), "AB": _sb(128), "OF": _sb(260), "OTF": _sb(8), "OT": _sb(8, "uint16"),
     "WH": _sb(132), "HB": _sb(1),
 }
 COUNTERS = ["v", "s", "p", "q"]
-DMAS = ["dx", "du", "da", "db", "dw", "w0", "w1", "w2", "w3", "o0", "o1", "o2", "o3", "o4", "o5", "o6"]
+DMAS = ["dx", "du", "da", "db", "dw", "w2", "w3", "o0", "o1", "o2", "o3", "o4", "o5", "o6"]
 SEMAPHORES = COUNTERS + DMAS + ["x1", "x2", "halo", "left"]
 AF = ActivationFunctionType
 ADD, SUB, MUL, MIN, MAX = AluOpType.add, AluOpType.subtract, AluOpType.mult, AluOpType.min, AluOpType.max
@@ -56,6 +85,10 @@ def view(name, c0=0, c1=None, p0=0, p1=128, step=1):
 
 def quarter(name, a, c0=0, c1=None, step=1):
     return view(name, c0, c1, 32 * a, 32 * a + 32, step)
+
+
+def half(name, h, c0=0, c1=None):
+    return view(name, c0, c1, 64 * h, 64 * h + 64)
 
 
 def width(w):
@@ -84,7 +117,7 @@ def accesses(o):
     return [(w, False) for w in o["rd"]] + [(w, True) for w in o["wr"]]
 
 
-def place(ops):
+def links(ops):
     n, log = len(ops), {}
     before = [dict() for _ in ops]
     last = None
@@ -105,18 +138,47 @@ def place(ops):
             if wr:
                 l[:] = [e for e in l if e[2] == i or not holds(w, e[0])]
             l.append((w, wr, i))
+    keys, seen = [], {}
+    for o in ops:
+        w = (o["wr"] or o["rd"])[0]
+        k = o.get("key") or "%s.%d.%d" % (w[0], w[1] // 32, w[3])
+        seen[k] = seen.get(k, 0) + 1
+        keys.append(k if seen[k] == 1 else "%s.%d" % (k, seen[k]))
+    return before, keys
+
+
+def place(ops, before, keys, table):
+    n = len(ops)
     after = [[] for _ in ops]
     for i in range(n):
         for j in before[i]:
             after[j].append(i)
+    missing = [len(b) for b in before]
+    ready = [i for i in range(n) if missing[i] == 0]
+    queue = [""] * n
+    if table:
+        rank = {}
+        for k, x in enumerate(table.split()):
+            x = x.split(":")
+            rank[x[0]] = (float(k), x[1])
+        at, order = [0.0] * n, []
+        for i in range(n):
+            at[i], queue[i] = rank.get(keys[i], (max([at[j] for j in before[i]], default=0.0) + 0.5, ops[i]["qs"][:1] or "-"))
+        while ready:
+            i = min(ready, key=lambda k: (at[k], k))
+            ready.remove(i)
+            order.append(i)
+            for k in after[i]:
+                missing[k] -= 1
+                if missing[k] == 0:
+                    ready.append(k)
+        return order, queue
     way = [0.0] * n
     for i in reversed(range(n)):
         o = ops[i]
         way[i] = o["cost"] + o["lag"] + max([way[k] + before[k][i] + OWN for k in after[i]], default=0.0)
-    missing = [len(b) for b in before]
-    ready = [i for i in range(n) if missing[i] == 0]
     busy = {}
-    start, end, queue = [0.0] * n, [0.0] * n, [""] * n
+    start, end = [0.0] * n, [0.0] * n
     while ready:
         i = max(ready, key=lambda k: (way[k], -k))
         ready.remove(i)
@@ -158,6 +220,9 @@ def rank_program(g, core, T, topo):
     def op(qs, fn, reads, writes, cost, sem=None, inc=1, local=True, lag=0.0):
         ops.append({"qs": qs, "fn": fn, "rd": reads, "wr": writes, "cost": cost, "sem": sem, "inc": inc, "local": local, "lag": lag})
 
+    def named(key):
+        ops[-1]["key"] = key
+
     def val(x):
         return ap(x) if isinstance(x, tuple) else x
 
@@ -188,8 +253,8 @@ def rank_program(g, core, T, topo):
             return e.activation(ap(o), ap(i), AF.Copy) if scale is None else e.activation(ap(o), ap(i), AF.Copy, scale=scale)
         op(qs, fn, [i], [o], time(width(i)))
 
-    def spread(o, x):
-        z = view("Z32", 0, 32, o[1], o[2])
+    def spread(o, x, z=None):
+        z = z or view("Z32", 0, 32, x[1], x[2])
 
         def fn(e, q):
             if q == "v":
@@ -212,14 +277,15 @@ def rank_program(g, core, T, topo):
             return e.activation(ap(j), ap(i), AF.Copy, accum_out=ap(o))
         op("vs", fn, [i], [o, j], time(width(i)) + 0.01)
 
-    def count(name, c0, i):
+    def count(name, c0, i, first=0.0):
         n, p0, p1, a, b, _ = i
         m = (a + b) // 2
         o, x, y = view(name, c0, c0 + m - a, p0, p1), view(n, a, m, p0, p1), view(n, m, b, p0, p1)
-        op("v", lambda e, q: e.tensor_tensor_scan(ap(o), ap(x), ap(y), 0.0, ADD, ADD), [x, y], [o], time(m - a, o, x))
+        op("v", lambda e, q: e.tensor_tensor_scan(ap(o), ap(x), ap(y), first, ADD, ADD), [x, y], [o], time(m - a, o, x))
 
     def signs(i, bias, acc, scale=1.0):
         act(waste(i), i, AF.Sign, bias=bias, scale=scale, acc=acc)
+        named("sg.%s.%d" % (acc[0], acc[3]))
 
     def tt(o, a, b, o0):
         op("v", lambda e, q: e.tensor_tensor(ap(o), ap(a), ap(b), o0), [a, b], [o], time(2 * width(a)))
@@ -230,9 +296,10 @@ def rank_program(g, core, T, topo):
     def turn(o, i):
         op("v", lambda e, q: e.transpose(ap(o), ap(i)), [i], [o], time(width(i)))
 
-    def swap(name, n):
-        copy(view(name, n, 2 * n, 64, 128), view(name, 0, n, 0, 64))
-        copy(view(name, n, 2 * n, 0, 64), view(name, 0, n, 64, 128))
+    def swap(name, n, both=False):
+        if both:
+            for h in (0, 1):
+                copy(half(name, h, n, 2 * n), half(name, 1 - h, 0, n))
         for a in range(4):
             copy(quarter(name, a, 2 * n, 4 * n), quarter(name, a ^ 1, 0, 2 * n))
 
@@ -251,14 +318,18 @@ def rank_program(g, core, T, topo):
     def load(q, name, dst, n, sem, more=0.0):
         o = view(dst, 0, n)
         op(q, lambda e, q: e.dma_start(ap(o), T[name][:, 0:n]), [], [o], 0.06, sem, 16, lag=LOCAL + more)
+        named("load." + name)
 
     def store(fn, i, sem):
         op("ys", lambda e, q: fn(e), [i], [], 0.06, sem, 16, lag=LOCAL)
+        named("store." + sem)
 
     def move(q, dst, d0, src, s0, n, s1, s2):
         o, i, os, is_ = view(dst, d0, d0 + n), view(src, s0, s0 + n), view("s" + dst, d0, d0 + n), view("s" + src, s0, s0 + n)
         op(q, lambda e, q: e.dma_start(ap(o).bitcast(dt.uint8), ap(i).bitcast(dt.uint8)), [i], [o], 0.06, s1, 16, lag=LOCAL)
+        named(s1)
         op(q, lambda e, q: e.dma_start(ap(os), ap(is_)), [is_], [os], 0.06, s2, 16, lag=LOCAL)
+        named(s2)
 
     others = [d for d in range(N) if d != r]
     where = [topo.addr(T.cores[d], core) for d in others]
@@ -267,14 +338,15 @@ def rank_program(g, core, T, topo):
         mask &= topo.mask(core, T.cores[d])
     lanes = bin(mask).count("1")
 
-    def to_all(src, land, k, sem):
+    def to_all(src, land, c0, k, sem):
         dsts = []
         for d in others:
             j = r if r < d else r - 1
-            dsts.append(T[land][:, k * j:k * j + k])
+            dsts.append(T[land][:, c0 + k * j:c0 + k * j + k])
         tr = RemoteDMATransfer(dst_ids=[DstId(rid=int(a), pnc=int(b)) for a, b in where], dma_engine_mask=mask,
                                remote_sem=T.sem[sem], srcs=[ap(src)], dsts=dsts, alu_op=0)
         op("q", lambda e, q: e.remote_dma_fused([tr], local_sem=T.sem.left), [src], [], 1.0, "left", lanes, False, FLY)
+        named("send." + sem)
 
     def to_one(d, d0, s0, n):
         rid, pid = topo.addr(T.cores[d], core)
@@ -283,14 +355,16 @@ def rank_program(g, core, T, topo):
         c, s = view("SRC", s0, s0 + n), view("sSRC", s0, s0 + n)
         oc, os = T.SRC[:, d0:d0 + n].bitcast(dt.uint8), T.sSRC[:, d0:d0 + n]
         op("q", lambda e, q: e.remote_dma(oc, ap(c).bitcast(dt.uint8), T.sem.halo, T.sem.left, pid, rid, m), [c], [], 0.7, "left", ln, False, FLY)
+        named("codes.%d" % (d > r))
         op("q", lambda e, q: e.remote_dma(os, ap(s), T.sem.halo, T.sem.left, pid, rid, m), [s], [], 0.7, "left", ln, False, FLY)
+        named("scales.%d" % (d > r))
 
     def arrive(sem, n, writes):
         ops.append({"qs": "", "fn": None, "rd": [], "wr": writes, "cost": 0.0, "sem": sem, "inc": n, "local": False, "lag": 0.0,
-                    "behind": max(k for k, o in enumerate(ops) if o["sem"] == "left")})
+                    "behind": max(k for k, o in enumerate(ops) if o["sem"] == "left"), "key": "come." + sem})
 
-    load("s", "u", "UC", 4, "du")
-    load("y", "x", "XT", 4 * P, "dx", 0.5)
+    load("s", "u", "U0", 8, "du")
+    load("y", "x", "XT", 4 * P, "dx", 0.0)
     load("y", "a", "AT", 2048, "da", 2.0)
     load("s", "b", "BT", 2048, "db", 2.0)
     load("y", "w", "WT", 512, "dw", 2.0)
@@ -298,6 +372,7 @@ def rank_program(g, core, T, topo):
     op("q", lambda e, q: e.iota(T.FI[:], [[1, 96]], 0, 0, allow_small_or_imprecise_dtypes=True), [], [view("FI")], 0.37)
     fill(view("Z32"), 0.0)
     fill(view("ZB"), 0.0)
+    fill(view("U0", 8, 512), 0.0)
     fill(view("XT", 4 * P, 512), 0.0)
     op("v", lambda e, q: e.tensor_scalar(T.PM[:, 0:1], T.PI[:], 31, None, AluOpType.bitwise_and), [view("PI")], [view("PM", 0, 1)], time(1))
     op("v", lambda e, q: e.tensor_scalar(T.PM[:, 1:2], T.PI[:], 15, None, AluOpType.bitwise_and), [view("PI")], [view("PM", 1, 2)], time(1))
@@ -307,22 +382,23 @@ def rank_program(g, core, T, topo):
     tt(view("PA"), view("PF"), view("X32"), SUB)
     tt(view("XA"), view("X32"), view("PA"), SUB)
     tt(view("PB"), view("PA"), view("X16"), ADD)
-    alpha, beta, sigma = (4, 6, 2, 2), (3, 2, 1, 1), (1, 3, 1, 2)
+    alpha, beta, sigma = (BA - 1, BB, 2, 2), (AA, AB - 2, 1, 1), (1, 3, 1, 2)
     for a in range(4):
-        for buf, c, v in (("KAP", 0, 4.0 * P * r + sigma[a]), ("FC", 0, 2.0 - 0.5 * sigma[a] + 127.0), ("WC", 0, 2.0 * P * alpha[a]),
+        for buf, c, v in (("KAP", 0, (4.0 * P * r + sigma[a]) * UNIT), ("FC", 0, 2.0 - 0.5 * sigma[a] + 127.0), ("WC", 0, 2.0 * P * alpha[a]),
                           ("WC", 1, 2.0 * P * beta[a]), ("WC", 2, float(sigma[a])), ("WC", 3, -2.0 * P * beta[a])):
             act(quarter(buf, a, c, c + 1), quarter("Z32", a, 0, 1), bias=v)
-        act(quarter("THR", a), quarter("Z32", a), bias=-BIG * (K - 0.5 if a < 3 else 1000.0))
-    for t in range(4):
-        ts(view("UT", t, 512, step=4), view("ZB"), view("UC", t, t + 1), ADD)
-    quant("QU", 0, 128, "UT")
+        act(quarter("THR", a), quarter("Z32", a), bias=0.5 - K if a < 3 else -1000.0)
+    quant("QV", 0, 128, "U0")
     quant("SRC", 0, 128, "XT")
 
-    mm(0, "SRC", 0, "QU", 0, 128)
-    mm(1, "QU", 0, "SRC", 0, 128)
+    mm(0, "SRC", 0, "QV", 0, 128)
     copy(view("X1S"), bank(0, 1))
+    for t in range(4):
+        ts(view("UT", t, 512, step=4), view("ZB"), view("U0", t, t + 1), ADD)
+    quant("QU", 0, 128, "UT")
+    mm(1, "QU", 0, "SRC", 0, 128)
     copy(view("SROW"), bank(1, 96))
-    to_all(view("X1S"), "X1L", 1, "x1")
+    to_all(view("X1S"), "X1L", 0, 1, "x1")
     arrive("x1", 7 * lanes, [view("X1L")])
     if r < N - 1:
         to_one(r + 1, H0, P - (56 - 8 * r), 56 - 8 * r)
@@ -336,7 +412,6 @@ def rank_program(g, core, T, topo):
         land += [view("SRC", H0 + 64 - 8 * r, H0 + HN), view("sSRC", H0 + 64 - 8 * r, H0 + HN)]
         cnt += 2 * bin(topo.mask(T.cores[r + 1], core)).count("1")
     arrive("halo", cnt, land)
-    move("y", "SRC", H0 - 56, "SRC", 0, 56, "w0", "w1")
     if r == 0:
         move("y", "SRC", H0, "SRC", 0, 64, "w2", "w3")
     if r == N - 1:
@@ -361,68 +436,80 @@ def rank_program(g, core, T, topo):
         ts(view("OE", 32 * b, 32 * b + 32), view("SQ"), s, EQ)
         ts(view("CM", o + 224, o + 256), view("SQ"), s, GT)
         tt(view("CM", o + 256, o + 288), view("OE", 32 * b, 32 * b + 32), view("TRI", 32 * b, 32 * b + 32), MUL)
+    count("CN", 288, view("CM", 800, 864), 32.0 * r)
     copy(view("JC"), view("X32"))
     ts(quarter("JC", 2), quarter("X32", 2), 32.0, ADD)
-    ts(view("KV"), view("FI"), 4.0, MUL, view("KAP"), ADD)
+    ts(view("KV"), view("FI"), 4.0 * UNIT, MUL, view("KAP"), ADD)
     fill(quarter("VR", 3), -HUGE)
     copy(quarter("VR", 2), quarter("SROW", 2))
     quant("SRC", P, 2 * P, "KT")
     mm(0, "QU", 0, "SRC", P, 2 * P)
     copy(quarter("VR", 0), bank(0, 96, 0, 32))
     copy(quarter("VR", 1), bank(0, 96, 32, 64, 96))
+
     for i in range(4):
-        mm(1 + i, "QA", 128 * i, "SRC", P, 2 * P)
+        mm(1 + i, "QA", 128 * i, "SRC", P, 2 * P + HN)
     for i in range(4):
-        mm((5 + i) % 8, "QB", 128 * i, "SRC", P, 2 * P)
-    for i in range(4):
-        copy(view("GO", i, 768, step=4), bank(1 + i, 192), 0.0625)
+        mm((5 + i) % 8, "QB", 128 * i, "SRC", P, 2 * P + HN)
+    fill(view("HK", 4 * HN, 4 * P), 0.0)
+    for i in range(8):
+        e0 = 4 * P * (i // 4)
+        copy(view("HK", e0 + i % 4, e0 + 4 * HN, step=4), bank((1 + i) % 8, HN, c0=2 * P), 0.0625)
+    for i in range(8):
+        e0 = 768 * (i // 4)
+        copy(view("GO", e0 + i % 4, e0 + 768, step=4), bank((1 + i) % 8, 2 * P), 0.0625)
+    quant("SRC", H0 + P, P + HN, "HK")
 
     for j in range(N - 1):
         spread(view("EX1", 32 * j, 32 * j + 32), view("X1L", j, j + 1))
     turn(view("R1"), view("EX1"))
-    for b in range(3):
+    for b in range(2):
         s, o = view("TS", 32 * b, 32 * b + 1), 288 * b
         if r > 0:
             ts(view("CM", o, o + 32 * r), view("R1", 0, 32 * r), s, GE)
+            named("GE.%d" % b)
         if r < N - 1:
             ts(view("CM", o + 32 * r, o + 224), view("R1", 32 * r, 224), s, GT)
+            named("GT.%d" % b)
         count("CN", 144 * b, view("CM", o, o + 288))
-    copy(quarter("CA", 0, 0, 3), quarter("CN", 1, 143, 432, 144))
-    copy(quarter("CA", 0, 3, 6), quarter("CN", 2, 143, 432, 144))
+    act(view("TG"), view("R1"), AF.Sign, bias=view("TS", 64, 65), scale=-1.0)
+    if r > 0:
+        act(waste(view("TG", 0, 32 * r)), view("TG", 0, 32 * r), AF.Relu, acc=view("TA", 0, 1))
+        named("TA.0")
+    else:
+        fill(view("TA", 0, 1), 0.0)
+    if r < N - 1:
+        act(waste(view("TG", 32 * r, 224)), view("TG", 32 * r, 224), AF.Relu, scale=-1.0, acc=view("TA", 1, 2))
+        named("TA.1")
+    else:
+        fill(view("TA", 1, 2), 0.0)
+    ts(view("CN", 431, 432), view("CN", 319, 320), view("TA", 0, 1), SUB, view("TA", 1, 2), ADD)
+    for a in (0, 1):
+        copy(quarter("CA", a, 0, 3), quarter("CN", 1 - a, 143, 432, 144))
+        copy(quarter("CA", a, 3, 6), quarter("CN", 2, 143, 432, 144))
     for b in range(3):
-        spread(quarter("E0", 0, 32 * b, 32 * b + 32), quarter("CN", 0, 144 * b + 143, 144 * b + 144))
-        ts(quarter("EX3", 0, 32 * b, 32 * b + 32), quarter("E0", 0, 32 * b, 32 * b + 32), quarter("CA", 0, b, b + 1), ADD,
-           quarter("CA", 0, 3 + b, 4 + b), ADD)
-    turn(quarter("PR", 0), quarter("EX3", 0))
-    for a in (1, 2, 3):
-        copy(quarter("PR", a), quarter("PR", 0))
+        spread(half("E0", 0, 32 * b, 32 * b + 32), half("CN", 0, 144 * b + 143, 144 * b + 144))
+        ts(half("EX3", 0, 32 * b, 32 * b + 32), half("E0", 0, 32 * b, 32 * b + 32), half("CA", 0, b, b + 1), ADD,
+           half("CA", 0, 3 + b, 4 + b), ADD)
+    turn(half("PR", 0), half("EX3", 0))
+    turn(half("PR", 1), half("EX3", 0))
     ts(view("OH"), view("PR"), view("JC"), EQ)
     tt(view("M2"), view("OH"), view("KV"), MUL)
     sums(view("XS", 1, 2), view("M2"))
     tt(view("M1"), view("OH"), view("VR"), MUL)
     sums(view("XS", 0, 1), view("M1"))
-    to_all(view("XS"), "X2L", 2, "x2")
-    arrive("x2", 7 * lanes, [view("X2L")])
+    to_all(view("XS"), "X2L", 4, 2, "x2")
+    arrive("x2", 7 * lanes, [view("X2L", 4, 18)])
 
-    for i in range(4):
-        mm(1 + i, "QA", 128 * i, "SRC", H0 - 56, 128)
-    for i in range(4):
-        copy(view("GO", 768 + i, 1536, step=4), bank((5 + i) % 8, 192), 0.0625)
-    for i in range(4):
-        mm((5 + i) % 8, "QB", 128 * i, "SRC", H0 - 56, 128)
-    fill(view("HK", 4 * HN, 4 * P), 0.0)
-    fill(view("HG", 4 * 168, 4 * 192), 0.0)
-    for i in range(8):
-        e0 = 4 * P * (i // 4)
-        copy(view("HK", e0 + i % 4, e0 + 4 * HN, step=4), bank((1 + i) % 8, HN, c0=56), 0.0625)
-    quant("SRC", H0 + P, P + HN, "HK")
+    fill(view("X2L", 2, 4), 0.0)
+    copy(view("X2L", 0, 2), view("XS"))
     for i in range(8):
         mm((1 + i) % 8, "QA" if i < 4 else "QB", 128 * (i % 4), "SRC", H0 + P, P + HN)
-    for i in range(3):
-        quant("SRC", 3 * P + 128 * i, 128, "GO", 512 * i)
+    quant("SRC", AA * P, 2 * P, "GO")
+    quant("SRC", BA * P, 2 * P, "GO", 768)
     for h in range(2):
         ts(view("PC", h, h + 1), view("PB"), 16.0 * h, ADD, E - 1.0, MIN)
-    swap("WC", 4)
+    swap("WC", 4, True)
     act(view("P2"), view("PC"), bias=2.0 * E * r, scale=2.0)
     act(view("PN"), view("PC"), bias=2.0 * E * r + 2.0, scale=2.0)
     act(view("NN"), view("PC", 1, 2), bias=-2.0 * E * r - 2.0, scale=-2.0)
@@ -438,32 +525,39 @@ def rank_program(g, core, T, topo):
         fill(view("W", 259, 528, step=264), 0.0)
     quant("QW", 0, 128, "WT")
     for i in range(8):
-        e0 = 4 * 192 * (i // 4)
-        copy(view("HG", e0 + i % 4, e0 + 4 * 168, step=4), bank((1 + i) % 8, 168), 0.0625)
-    for i in range(2):
-        quant("SRC", H0 + 3 * P + 180 * i, 180, "HG", 720 * i)
+        e0 = 672 * (i // 4)
+        copy(view("HG", e0 + i % 4, e0 + 672, step=4), bank((1 + i) % 8, P + HN), 0.0625)
+    quant("SRC", H0 + AA * P, P + HN, "HG")
+    quant("SRC", H0 + BA * P, P + HN, "HG", 672)
 
-    sc, mc = view("EX2", 0, 1), view("EX2", 32, 33)
+    sc, mc = view("EX2", 0, 1), view("EX2", 64, 65)
     for k, row in ((0, "DS"), (1, "DN")):
-        sums(view("SC", k, k + 1), view("X2L", k, 14, step=2))
-        ts(view("EX2", 32 * k, 32 * k + 32), view("Z32"), view("SC", k, k + 1), ADD, view("XS", k, k + 1), ADD)
-        turn(view(row, 0, 32), view("EX2", 32 * k, 32 * k + 32))
+        sums(view("SC", k, k + 1), view("X2L", k, 18, step=2))
+        spread(view("EX2", 64 * k, 64 * k + 32), view("SC", k, k + 1))
+        for h in (0, 1):
+            spread(half("EX2", h, 64 * k + 32, 64 * k + 64), half("SC", 1 - h, k, k + 1))
+        turn(view(row, 0, 64), view("EX2", 64 * k, 64 * k + 64))
         swap(row, 32)
     act(view("SG"), view("DS"), AF.Sign, bias=sc, scale=-1.0)
     ts(view("LO"), view("DN"), mc, GE, -0.5, MUL)
     tt(view("BF"), view("SG"), view("LO"), LE)
-    act(waste(view("BF")), view("BF"), scale=BIG, acc=view("P1"))
-    ts(view("EXM"), view("THR"), view("P1"), ADD, mc, MAX)
+    count("P1", 0, view("BF"))
+    ts(view("EXM"), view("THR"), view("P1", 63, 64), ADD, mc, MAX)
     turn(view("MR", 0, 32), view("EXM"))
+    for h in (0, 1):
+        turn(half("MR", h, 32, 64), half("EXM", 1 - h))
     swap("MR", 32)
     signs(view("MR"), view("EXM", 0, 1), view("RK"), -1.0)
-    ts(view("F0"), view("EXM", 0, 1), 0.5, MUL, view("FC"), ADD)
+    ts(view("F0"), view("EXM", 0, 1), 0.5 / UNIT, MUL, view("FC"), ADD)
+    spread(view("F32"), view("F0"))
     if r > 0:
-        signs(view("MR"), 4.0 * P * r - 0.5, view("SB", 0, 1), -1.0)
+        signs(view("MR"), (4.0 * P * r - 0.5) * UNIT, view("SB", 0, 1), -1.0)
     if r < N - 1:
-        signs(view("MR"), 4.0 * P * (r + 1) - 0.5, view("SB", 1, 2), -1.0)
-    ts(view("EXF"), view("Z32"), view("RK"), ADD, view("F0"), ADD)
-    turn(view("FR", 0, 32), view("EXF"))
+        signs(view("MR"), (4.0 * P * (r + 1) - 0.5) * UNIT, view("SB", 1, 2), -1.0)
+    spread(view("EXF", 0, 32), view("RK"), view("F32"))
+    for h in (0, 1):
+        spread(half("EXF", h, 32, 64), half("RK", 1 - h), half("F32", 1 - h))
+    turn(view("FR", 0, 64), view("EXF"))
     swap("FR", 32)
 
     for h in range(2):
@@ -474,8 +568,10 @@ def rank_program(g, core, T, topo):
         act(view("W", c, c + 32), view("AB", 32 * k, 32 * k + 32), AF.Relu, bias=view("WC", 4 * k + 1, 4 * k + 2), scale=view("WC", 4 * k + 3, 4 * k + 4))
     if r > 0:
         ts(view("W", 258, 528, step=264), view("W", 256, 528, step=264), view("SB", 0, 1), LT, 2.0 * (H0 + 64 - 8 * r), MUL)
+        named("low")
     if r < N - 1:
         ts(view("W", 259, 528, step=264), view("W", 260, 528, step=264), view("SB", 1, 2), GE, 2.0 * (H0 - 32 - 8 * r), MUL)
+        named("high")
     for h in range(2):
         for k in range(4):
             f, c = view("FR", 32 * k, 32 * k + 32), 264 * h + 32 * k
@@ -506,7 +602,7 @@ def rank_program(g, core, T, topo):
     sums(view("HB"), view("WH", 0, 131))
     store(lambda e: e.dma_start(T.hs[0:1, 0:E], T.HB[0:E, 0:1]), view("HB", 0, 1, 0, E), "o6")
 
-    order, queue = place(ops)
+    order, queue = place(ops, *links(ops), ORDER)
     total = {}
     known = {k: {} for k in queues}
     clocks = {}

from concourse.bass import DstId, RemoteDMATransfer
from concourse.mybir import dt, AluOpType, AxisListType, ActivationFunctionType

N, P, K = 8, 96, 32
E = P + 2 * K // N
AA, AB, BA, BB = 6, 7, 11, 12
H0 = 3 * P
HN = 72
ALL = H0 + BB * P + HN
UNIT = 2.0 ** -20
HUGE = 1.0e29
CODE = "float8_e4m3fn_x4"
HALF = "bfloat16"
CYCLE, SYNC, OWN, FLY, LOCAL = 0.0009, 0.16, 0.14, 1.6, 2.0
ORDER = """
load.u:s XT.0.384:v load.x:y Z32.0.0:v U0.0.8:v load.a:y KAP.3.0:s PI.0.0:q PM.0.1:v KAP.0.0:s VR.3.0:v THR.2.0:s ZB.0.0:v
PF.0.0:v PM.0.0:v X16.0.0:v WC.1.2:s load.b:s X32.0.0:v PA.0.0:v QV.0.0:v load.w:y KAP.1.0:s WC.1.0:s SRC.0.0:v WC.1.1:s
HK.0.288:v FI.0.0:q UT.0.3:v UT.0.1:v WC.2.3:s WC.3.2:s JC.0.0:s ps.0.0:p X1S.0.0:s KAP.2.0:s UT.0.0:v UT.0.2:v XA.0.0:v
WC.0.0:s XB.0.0:v QU.0.0:v XB.0.2:v PB.0.0:v H2.0.0:s X2L.0.2:v ps.0.512:p XB.0.1:v SROW.0.0:s KV.0.0:v send.x1:q PC.0.0:v
FC.1.0:s WC.1.3:s WC.2.2:s SQ.0.0:s PC.0.1:v WC.3.1:s TS.0.0:v THR.0.0:s WH.0.128:s WC.3.3:s JC.2.0:v codes.1:q WC.0.2:s
SQ.2.0:s scales.1:q TRI.0.32:v QA.0.0:v QB.0.0:v WC.0.1:s SQ.3.0:v WC.3.0:s SQ.1.0:s ps.0.1024:p WC.2.1:s KT.0.2:s ps.0.1536:p
OE.0.32:v OE.0.64:v ps.0.0.2:p VR.2.0:s ps.0.3584:p ps.0.3072:p FC.2.0:s KT.0.3:s WC.0.3:s TRI.0.64:v FC.3.0:s CM.0.512:v
W.0.256:s codes.0:q OE.0.0:v CM.0.544:v TRI.0.0:v KT.0.0:v come.x1:- WC.2.4:s KT.0.387:s CM.0.800:v CM.0.224:v ps.0.2560:p
CM.0.832:v CM.0.256:v EX1.0.192:v NS.0.0:s EX1.0.64:s ps.0.2048:p EX1.0.32:v EX1.0.96:s KT.0.386:s P2.0.0:s EX1.0.160:v
ps.0.512.2:p FC.0.0:s KT.0.385:s EX1.0.0:v KT.0.384:s EX1.0.128:v KT.0.1:s R1.0.0:v WC.2.8:s CN.0.288:v GE.0:v GE.1:v
scales.0:q SRC.0.96:v TG.0.0:s TA.1:s TA.0:s GT.0:v W.0.260:s WC.2.0:s GT.1:v NH.0.0:s CN.0.0:v WC.0.4:s CN.0.144:v E0.0.0:s
CN.0.431:v CA.0.0:v CA.1.3:v CA.0.3:v ps.0.0.3:p CA.1.0:v E0.0.32:s PN.0.0:s WC.3.8:s THR.1.0:s E0.0.64:v VR.0.0:s EX3.0.0:v
VR.1.0:s EX3.0.64:v EX3.0.32:v PR.2.0:v PR.0.0:v OH.0.0:v come.halo:- THR.3.0:s M2.0.0:v M1.0.0:v ps.0.2048.2:p ps.0.512.3:p
XS.0.0:v ps.0.1536.2:p XS.0.1:s HK.0.2:v ps.0.3584.2:p WC.0.8:v HK.0.0:s X2L.0.0:s HK.0.386:s HK.0.3:v ps.0.1024.2:p
ps.0.3072.2:p ps.0.2560.2:p GO.0.2:s WC.1.8:s NN.0.0:s ps.0.0.4:p send.x2:q HK.0.1:v GO.0.0:s HK.0.385:s GO.0.1:v GO.0.3:s
QW.0.0:v HK.0.384:s GO.0.769:s GO.0.770:v SRC.0.576:v come.x2:- HK.0.387:v SRC.0.384:v SC.0.0:s SC.0.1:s GO.0.771:v EX2.0.32:v
EX2.2.32:s EX2.0.0:s EX2.2.96:s EX2.0.96:v EX2.0.64:s DS.0.0:v GO.0.768:s ps.0.1536.3:p DS.1.64:s ps.0.3072.3:p DS.3.64:s
DN.0.0:v ps.0.2048.3:p DS.0.64:v DN.0.64:s ps.0.1024.3:p DN.3.64:s DS.2.64:v SG.0.0:s DN.1.64:v DN.2.64:v SRC.0.1056:v LO.0.0:v
ps.0.512.4:p HG.0.2:s HG.0.3:s HG.0.1:s BF.0.0:v P1.0.0:v HG.0.673:s HG.0.0:s EXM.0.0:v MR.0.0:v ps.0.2560.3:p MR.2.32:v
HG.0.672:s MR.0.32:v F0.0.0:v MR.3.64:v MR.1.64:v F32.0.0:v MR.2.64:s ps.0.3584.3:p MR.0.64:s ps.0.0.5:p HG.0.674:s sg.RK.0:s
EXF.2.32:s EXF.0.32:s SRC.0.864:v HG.0.675:v EXF.0.0:s SRC.0.1344:v FR.0.0:v FR.2.64:v FR.0.64:v sg.SB.1:s sg.SB.0:s FR.3.64:s
FR.1.64:s W.0.32:v high:v low:v W.0.0:v W.0.264:v AB.0.0:s W.0.360:v sg.W.257:s W.0.392:s W.0.192:v W.0.96:v W.0.160:v
W.0.224:v W.0.64:v W.0.128:v W.0.328:v sg.W.521:s W.0.488:s W.0.424:s W.0.296:v OF.0.0:v W.0.456:s OF.0.130:v WH.0.0:v
OTF.2.6:v OTF.0.0:s OTF.2.0:v OTF.2.4:s OTF.0.2:v OTF.0.6:s OTF.1.4:v OTF.1.6:s OTF.2.2:s OTF.3.0:s OTF.0.4:v OTF.1.2:v
OTF.3.4:v OTF.1.0:s OTF.3.2:v OTF.3.6:v OT.0.0:v sg.WH.129:s sRUN.0.0:s sg.WH.130:s RUN.0.0:v WH.0.64:v WH.0.96:v WH.0.32:v
store.o2:y ps.0.0.6:p store.o4:s store.o3:y store.o1:y HB.0.0:s YT.0.0:s store.o5:s store.o0:y store.o6:y
"""


def _sb(n, d="float32"):
    return ("sbuf", [128, n], d)


SCRATCH = {
    "XT": _sb(512, HALF), "U0": _sb(512, HALF), "UT": _sb(512, HALF), "ZB": _sb(128, HALF),
    "AT": _sb(2048, HALF), "BT": _sb(2048, HALF), "WT": _sb(512, HALF),
    "QU": _sb(128, CODE), "sQU": _sb(128, "uint8"), "QV": _sb(128, CODE), "sQV": _sb(128, "uint8"),
    "QA": _sb(512, CODE), "sQA": _sb(512, "uint8"), "QB": _sb(512, CODE), "sQB": _sb(512, "uint8"),
    "QW": _sb(128, CODE), "sQW": _sb(128, "uint8"),
    "SRC": _sb(ALL, CODE), "sSRC": _sb(ALL, "uint8"),
    "KT": _sb(768, HALF), "GO": _sb(1536, HALF), "HK": _sb(672, HALF), "HG": _sb(1344, HALF),
    "RUN": _sb(128, CODE), "sRUN": _sb(128, "uint8"), "YT": _sb(E),
    "ps": ("psum", [128, 4096], "float32"),
    "Z32": _sb(32), "PI": _sb(1, "int32"), "PM": _sb(2, "int32"), "PF": _sb(1), "X32": _sb(1), "X16": _sb(1),
    "FI": _sb(96), "XA": _sb(1), "XB": _sb(3), "TRI": _sb(96), "JC": _sb(1), "KAP": _sb(1), "KV": _sb(96), "VR": _sb(96), "FC": _sb(1),
    "PA": _sb(1), "PB": _sb(1), "PC": _sb(2), "P2": _sb(2), "PN": _sb(2), "NN": _sb(1), "NS": _sb(2), "H2": _sb(1), "NH": _sb(1),
    "WC": _sb(16), "THR": _sb(32),
    "X1S": _sb(1), "X1L": _sb(7), "SROW": _sb(96), "SQ": _sb(32), "TS": _sb(96), "OE": _sb(96),
    "EX1": _sb(224), "R1": _sb(224), "CM": _sb(864, HALF), "CN": _sb(432, HALF), "CA": _sb(6), "TG": _sb(224, HALF), "TA": _sb(2),
    "E0": _sb(96), "EX3": _sb(96), "PR": _sb(96), "OH": _sb(96), "M1": _sb(96), "M2": _sb(96),
    "XS": _sb(2), "X2L": _sb(20), "SC": _sb(2), "EX2": _sb(128), "DS": _sb(128), "DN": _sb(128), "SG": _sb(128, HALF), "LO": _sb(128, HALF),
    "BF": _sb(128, HALF), "P1": _sb(64), "EXM": _sb(32), "MR": _sb(128),
    "F0": _sb(1), "F32": _sb(32), "RK": _sb(1), "SB": _sb(2), "EXF": _sb(64), "FR": _sb(128), "J4": _sb(2304),
    "W": _sb(528), "AB": _sb(128), "OF": _sb(260), "OTF": _sb(8), "OT": _sb(8, "uint16"),
    "WH": _sb(132), "HB": _sb(1),
}
COUNTERS = ["v", "s", "p", "q"]
DMAS = ["dx", "du", "da", "db", "dw", "w2", "w3", "o0", "o1", "o2", "o3", "o4", "o5", "o6"]
SEMAPHORES = COUNTERS + DMAS + ["x1", "x2", "halo", "left"]
AF = ActivationFunctionType
ADD, SUB, MUL, MIN, MAX = AluOpType.add, AluOpType.subtract, AluOpType.mult, AluOpType.min, AluOpType.max
GT, GE, LT, LE, EQ = AluOpType.is_gt, AluOpType.is_ge, AluOpType.is_lt, AluOpType.is_le, AluOpType.is_equal


def view(name, c0=0, c1=None, p0=0, p1=128, step=1):
    if c1 is None:
        c1 = SCRATCH[name][1][1]
    return (name, p0, p1, c0, c1, step)


def quarter(name, a, c0=0, c1=None, step=1):
    return view(name, c0, c1, 32 * a, 32 * a + 32, step)


def half(name, h, c0=0, c1=None):
    return view(name, c0, c1, 64 * h, 64 * h + 64)


def width(w):
    return len(range(w[3], w[4], w[5]))


def meet(a, b):
    if a[1] >= b[2] or b[1] >= a[2] or a[3] >= b[4] or b[3] >= a[4]:
        return False
    if a[5] == 1 and b[5] == 1:
        return True
    return bool(set(range(a[3], a[4], a[5])) & set(range(b[3], b[4], b[5])))


def holds(a, b):
    return a[5] == 1 and a[1] <= b[1] and a[2] >= b[2] and a[3] <= b[3] and a[4] >= b[4]


def wide(w):
    if w[0] != "ps":
        return w
    return ("ps", 0, 128, w[3] // 512 * 512, (w[4] + 511) // 512 * 512, 1)


def accesses(o):
    return [(w, False) for w in o["rd"]] + [(w, True) for w in o["wr"]]


def links(ops):
    n, log = len(ops), {}
    before = [dict() for _ in ops]
    last = None
    for i, o in enumerate(ops):
        for w, wr in accesses(o):
            for v, vr, j in log.get(w[0], []):
                if j != i and (wr or vr or w[0] == "ps") and meet(wide(w), v):
                    before[i].setdefault(j, 0.0)
        if "behind" in o:
            before[i][o["behind"]] = 0.0
        if o["qs"] == "q":
            if last is not None:
                before[i].setdefault(last, -ops[last]["lag"])
            last = i
        for w, wr in accesses(o):
            w = wide(w)
            l = log.setdefault(w[0], [])
            if wr:
                l[:] = [e for e in l if e[2] == i or not holds(w, e[0])]
            l.append((w, wr, i))
    keys, seen = [], {}
    for o in ops:
        w = (o["wr"] or o["rd"])[0]
        k = o.get("key") or "%s.%d.%d" % (w[0], w[1] // 32, w[3])
        seen[k] = seen.get(k, 0) + 1
        keys.append(k if seen[k] == 1 else "%s.%d" % (k, seen[k]))
    return before, keys


def place(ops, before, keys, table):
    n = len(ops)
    after = [[] for _ in ops]
    for i in range(n):
        for j in before[i]:
            after[j].append(i)
    missing = [len(b) for b in before]
    ready = [i for i in range(n) if missing[i] == 0]
    queue = [""] * n
    if table:
        rank = {}
        for k, x in enumerate(table.split()):
            x = x.split(":")
            rank[x[0]] = (float(k), x[1])
        at, order = [0.0] * n, []
        for i in range(n):
            at[i], queue[i] = rank.get(keys[i], (max([at[j] for j in before[i]], default=0.0) + 0.5, ops[i]["qs"][:1] or "-"))
        while ready:
            i = min(ready, key=lambda k: (at[k], k))
            ready.remove(i)
            order.append(i)
            for k in after[i]:
                missing[k] -= 1
                if missing[k] == 0:
                    ready.append(k)
        return order, queue
    way = [0.0] * n
    for i in reversed(range(n)):
        o = ops[i]
        way[i] = o["cost"] + o["lag"] + max([way[k] + before[k][i] + OWN for k in after[i]], default=0.0)
    busy = {}
    start, end = [0.0] * n, [0.0] * n
    while ready:
        i = max(ready, key=lambda k: (way[k], -k))
        ready.remove(i)
        o, best = ops[i], None
        for q in o["qs"] or ["-"]:
            t = 0.0
            for j, gap in before[i].items():
                wake = 0.0 if q == "-" else SYNC if queue[j] != q else OWN if q in "vs" else 0.0
                t = max(t, end[j] + gap + wake)
            if q != "-":
                for s, e in busy.setdefault(q, []):
                    if t + o["cost"] <= s + 1e-9:
                        break
                    t = max(t, e)
            if best is None or t < best[0] - 1e-9:
                best = (t, q)
        start[i], queue[i] = best
        end[i] = start[i] + o["cost"] + o["lag"]
        if queue[i] != "-":
            busy[queue[i]] = sorted(busy[queue[i]] + [(start[i], start[i] + o["cost"])])
        for k in after[i]:
            missing[k] -= 1
            if missing[k] == 0:
                ready.append(k)
    return sorted(range(n), key=lambda i: (start[i], i)), queue


def rank_program(g, core, T, topo):
    r = T.rank_of(core)
    if r is None:
        return
    queues = {"v": g.vector, "s": g.scalar, "p": g.tensor, "q": g, "y": g.sync}
    ops = []

    def ap(w):
        n, p0, p1, c0, c1, st = w
        return T[n][p0:p1, c0:c1] if st == 1 else T[n][p0:p1, c0:c1:st]

    def op(qs, fn, reads, writes, cost, sem=None, inc=1, local=True, lag=0.0):
        ops.append({"qs": qs, "fn": fn, "rd": reads, "wr": writes, "cost": cost, "sem": sem, "inc": inc, "local": local, "lag": lag})

    def named(key):
        ops[-1]["key"] = key

    def val(x):
        return ap(x) if isinstance(x, tuple) else x

    def time(n, *sides):
        if sides and all(SCRATCH[w[0]][2] == HALF for w in sides):
            n = n / 2
        return max(64, n) * CYCLE

    def act(o, i, func=AF.Copy, bias=None, scale=None, acc=None):
        kw = {}
        for k, x in (("bias", bias), ("scale", scale), ("accum_out", acc)):
            if x is not None:
                kw[k] = val(x)
        op("s", lambda e, q: e.activation(ap(o), ap(i), func, **kw), [i] + [x for x in (bias, scale) if isinstance(x, tuple)],
           [o] + ([acc] if acc is not None else []), time(width(i)) + (0.025 if acc is not None else 0.0))

    def ts(o, i, s1, op0, s2=None, op1=None):
        rd = [i] + [s for s in (s1, s2) if isinstance(s, tuple)]
        if op1 is None:
            op("v", lambda e, q: e.tensor_scalar(ap(o), ap(i), val(s1), None, op0), rd, [o], time(width(i), o, i))
        else:
            op("v", lambda e, q: e.tensor_scalar(ap(o), ap(i), val(s1), val(s2), op0, op1), rd, [o], time(width(i), o, i))

    def copy(o, i, scale=None, qs="vs"):
        def fn(e, q):
            if q == "v":
                return e.tensor_copy(ap(o), ap(i)) if scale is None else e.tensor_scalar(ap(o), ap(i), scale, None, MUL)
            return e.activation(ap(o), ap(i), AF.Copy) if scale is None else e.activation(ap(o), ap(i), AF.Copy, scale=scale)
        op(qs, fn, [i], [o], time(width(i)))

    def spread(o, x, z=None):
        z = z or view("Z32", 0, 32, x[1], x[2])

        def fn(e, q):
            if q == "v":
                return e.tensor_scalar(ap(o), ap(z), ap(x), None, ADD)
            return e.activation(ap(o), ap(z), AF.Identity, bias=ap(x))
        op("vs", fn, [z, x], [o], time(32))

    junk = [0]

    def waste(i):
        junk[0] += width(i)
        return view("J4", junk[0] - width(i), junk[0], i[1], i[2])

    def sums(o, i):
        j = waste(i)

        def fn(e, q):
            if q == "v":
                return e.tensor_reduce(ap(o), ap(i), AxisListType.X, ADD)
            return e.activation(ap(j), ap(i), AF.Copy, accum_out=ap(o))
        op("vs", fn, [i], [o, j], time(width(i)) + 0.01)

    def count(name, c0, i, first=0.0):
        n, p0, p1, a, b, _ = i
        m = (a + b) // 2
        o, x, y = view(name, c0, c0 + m - a, p0, p1), view(n, a, m, p0, p1), view(n, m, b, p0, p1)
        op("v", lambda e, q: e.tensor_tensor_scan(ap(o), ap(x), ap(y), first, ADD, ADD), [x, y], [o], time(m - a, o, x))

    def signs(i, bias, acc, scale=1.0):
        act(waste(i), i, AF.Sign, bias=bias, scale=scale, acc=acc)
        named("sg.%s.%d" % (acc[0], acc[3]))

    def tt(o, a, b, o0):
        op("v", lambda e, q: e.tensor_tensor(ap(o), ap(a), ap(b), o0), [a, b], [o], time(2 * width(a)))

    def fill(o, c):
        op("v", lambda e, q: e.memset(ap(o), c), [], [o], time(width(o), o))

    def turn(o, i):
        op("v", lambda e, q: e.transpose(ap(o), ap(i)), [i], [o], time(width(i)))

    def swap(name, n, both=False):
        if both:
            for h in (0, 1):
                copy(half(name, h, n, 2 * n), half(name, 1 - h, 0, n))
        for a in range(4):
            copy(quarter(name, a, 2 * n, 4 * n), quarter(name, a ^ 1, 0, 2 * n))

    def quant(dst, c0, n, src, e0=0):
        o, s, i = view(dst, c0, c0 + n), view("s" + dst, c0, c0 + n), view(src, e0, e0 + 4 * n)
        op("v", lambda e, q: e.quantize_mx(ap(o), ap(s), ap(i)), [i], [o, s], 0.015 + 0.001 * n)

    def mm(bk, w, wc, x, xc, n):
        o = view("ps", 512 * bk, 512 * bk + n)
        a, sa, b, sb = view(w, wc, wc + 128), view("s" + w, wc, wc + 128), view(x, xc, xc + n), view("s" + x, xc, xc + n)
        op("p", lambda e, q: e.matmul_mx(ap(o), ap(a), ap(sa), ap(b), ap(sb), True, True), [a, sa, b, sb], [o], 1.3 * CYCLE * (n + 16))

    def bank(i, n, p0=0, p1=128, c0=0):
        return view("ps", 512 * i + c0, 512 * i + c0 + n, p0, p1)

    def load(q, name, dst, n, sem, more=0.0):
        o = view(dst, 0, n)
        op(q, lambda e, q: e.dma_start(ap(o), T[name][:, 0:n]), [], [o], 0.06, sem, 16, lag=LOCAL + more)
        named("load." + name)

    def store(fn, i, sem):
        op("ys", lambda e, q: fn(e), [i], [], 0.06, sem, 16, lag=LOCAL)
        named("store." + sem)

    def move(q, dst, d0, src, s0, n, s1, s2):
        o, i, os, is_ = view(dst, d0, d0 + n), view(src, s0, s0 + n), view("s" + dst, d0, d0 + n), view("s" + src, s0, s0 + n)
        op(q, lambda e, q: e.dma_start(ap(o).bitcast(dt.uint8), ap(i).bitcast(dt.uint8)), [i], [o], 0.06, s1, 16, lag=LOCAL)
        named(s1)
        op(q, lambda e, q: e.dma_start(ap(os), ap(is_)), [is_], [os], 0.06, s2, 16, lag=LOCAL)
        named(s2)

    others = [d for d in range(N) if d != r]
    where = [topo.addr(T.cores[d], core) for d in others]
    mask = topo.mask(core, T.cores[others[0]])
    for d in others:
        mask &= topo.mask(core, T.cores[d])
    lanes = bin(mask).count("1")

    def to_all(src, land, c0, k, sem):
        dsts = []
        for d in others:
            j = r if r < d else r - 1
            dsts.append(T[land][:, c0 + k * j:c0 + k * j + k])
        tr = RemoteDMATransfer(dst_ids=[DstId(rid=int(a), pnc=int(b)) for a, b in where], dma_engine_mask=mask,
                               remote_sem=T.sem[sem], srcs=[ap(src)], dsts=dsts, alu_op=0)
        op("q", lambda e, q: e.remote_dma_fused([tr], local_sem=T.sem.left), [src], [], 1.0, "left", lanes, False, FLY)
        named("send." + sem)

    def to_one(d, d0, s0, n):
        rid, pid = topo.addr(T.cores[d], core)
        m = topo.mask(core, T.cores[d])
        ln = bin(m).count("1")
        c, s = view("SRC", s0, s0 + n), view("sSRC", s0, s0 + n)
        oc, os = T.SRC[:, d0:d0 + n].bitcast(dt.uint8), T.sSRC[:, d0:d0 + n]
        op("q", lambda e, q: e.remote_dma(oc, ap(c).bitcast(dt.uint8), T.sem.halo, T.sem.left, pid, rid, m), [c], [], 0.7, "left", ln, False, FLY)
        named("codes.%d" % (d > r))
        op("q", lambda e, q: e.remote_dma(os, ap(s), T.sem.halo, T.sem.left, pid, rid, m), [s], [], 0.7, "left", ln, False, FLY)
        named("scales.%d" % (d > r))

    def arrive(sem, n, writes):
        ops.append({"qs": "", "fn": None, "rd": [], "wr": writes, "cost": 0.0, "sem": sem, "inc": n, "local": False, "lag": 0.0,
                    "behind": max(k for k, o in enumerate(ops) if o["sem"] == "left"), "key": "come." + sem})

    load("s", "u", "U0", 8, "du")
    load("y", "x", "XT", 4 * P, "dx", 0.0)
    load("y", "a", "AT", 2048, "da", 2.0)
    load("s", "b", "BT", 2048, "db", 2.0)
    load("y", "w", "WT", 512, "dw", 2.0)
    op("q", lambda e, q: e.iota(T.PI[:], [[0, 1]], 0, 1), [], [view("PI")], 0.16)
    op("q", lambda e, q: e.iota(T.FI[:], [[1, 96]], 0, 0, allow_small_or_imprecise_dtypes=True), [], [view("FI")], 0.37)
    fill(view("Z32"), 0.0)
    fill(view("ZB"), 0.0)
    fill(view("U0", 8, 512), 0.0)
    fill(view("XT", 4 * P, 512), 0.0)
    op("v", lambda e, q: e.tensor_scalar(T.PM[:, 0:1], T.PI[:], 31, None, AluOpType.bitwise_and), [view("PI")], [view("PM", 0, 1)], time(1))
    op("v", lambda e, q: e.tensor_scalar(T.PM[:, 1:2], T.PI[:], 15, None, AluOpType.bitwise_and), [view("PI")], [view("PM", 1, 2)], time(1))
    copy(view("PF"), view("PI"), qs="v")
    copy(view("X32"), view("PM", 0, 1), qs="v")
    copy(view("X16"), view("PM", 1, 2), qs="v")
    tt(view("PA"), view("PF"), view("X32"), SUB)
    tt(view("XA"), view("X32"), view("PA"), SUB)
    tt(view("PB"), view("PA"), view("X16"), ADD)
    alpha, beta, sigma = (BA - 1, BB, 2, 2), (AA, AB - 2, 1, 1), (1, 3, 1, 2)
    for a in range(4):
        for buf, c, v in (("KAP", 0, (4.0 * P * r + sigma[a]) * UNIT), ("FC", 0, 2.0 - 0.5 * sigma[a] + 127.0), ("WC", 0, 2.0 * P * alpha[a]),
                          ("WC", 1, 2.0 * P * beta[a]), ("WC", 2, float(sigma[a])), ("WC", 3, -2.0 * P * beta[a])):
            act(quarter(buf, a, c, c + 1), quarter("Z32", a, 0, 1), bias=v)
        act(quarter("THR", a), quarter("Z32", a), bias=0.5 - K if a < 3 else -1000.0)
    quant("QV", 0, 128, "U0")
    quant("SRC", 0, 128, "XT")

    mm(0, "SRC", 0, "QV", 0, 128)
    copy(view("X1S"), bank(0, 1))
    for t in range(4):
        ts(view("UT", t, 512, step=4), view("ZB"), view("U0", t, t + 1), ADD)
    quant("QU", 0, 128, "UT")
    mm(1, "QU", 0, "SRC", 0, 128)
    copy(view("SROW"), bank(1, 96))
    to_all(view("X1S"), "X1L", 0, 1, "x1")
    arrive("x1", 7 * lanes, [view("X1L")])
    if r < N - 1:
        to_one(r + 1, H0, P - (56 - 8 * r), 56 - 8 * r)
    if r > 0:
        to_one(r - 1, H0 + HN - 8 * r, 0, 8 * r)
    land, cnt = [], 0
    if r > 0:
        land += [view("SRC", H0, H0 + 64 - 8 * r), view("sSRC", H0, H0 + 64 - 8 * r)]
        cnt += 2 * bin(topo.mask(T.cores[r - 1], core)).count("1")
    if r < N - 1:
        land += [view("SRC", H0 + 64 - 8 * r, H0 + HN), view("sSRC", H0 + 64 - 8 * r, H0 + HN)]
        cnt += 2 * bin(topo.mask(T.cores[r + 1], core)).count("1")
    arrive("halo", cnt, land)
    if r == 0:
        move("y", "SRC", H0, "SRC", 0, 64, "w2", "w3")
    if r == N - 1:
        move("y", "SRC", H0 + 8, "SRC", 0, 64, "w2", "w3")

    turn(view("TS"), view("SROW"))
    for a in range(4):
        copy(quarter("SQ", a), quarter("SROW", a, 32 * (a % 3), 32 * (a % 3) + 32))
    quant("QA", 0, 512, "AT")
    for i in range(4):
        mm(i, "QA", 128 * i, "SRC", 0, 128)
    quant("QB", 0, 512, "BT")
    for i in range(4):
        mm(4 + i, "QB", 128 * i, "SRC", 0, 128)
    for i in range(8):
        copy(view("KT", i % 4 + 384 * (i // 4), 384 + 384 * (i // 4), step=4), bank(i, 96), 0.0625)
    for b in range(3):
        ts(view("XB", b, b + 1), view("XA"), 32.0 * b, ADD)
    for b in range(3):
        s, o = view("TS", 32 * b, 32 * b + 1), 288 * b
        ts(view("TRI", 32 * b, 32 * b + 32), view("FI", 0, 32), view("XB", b, b + 1), LT)
        ts(view("OE", 32 * b, 32 * b + 32), view("SQ"), s, EQ)
        ts(view("CM", o + 224, o + 256), view("SQ"), s, GT)
        tt(view("CM", o + 256, o + 288), view("OE", 32 * b, 32 * b + 32), view("TRI", 32 * b, 32 * b + 32), MUL)
    count("CN", 288, view("CM", 800, 864), 32.0 * r)
    copy(view("JC"), view("X32"))
    ts(quarter("JC", 2), quarter("X32", 2), 32.0, ADD)
    ts(view("KV"), view("FI"), 4.0 * UNIT, MUL, view("KAP"), ADD)
    fill(quarter("VR", 3), -HUGE)
    copy(quarter("VR", 2), quarter("SROW", 2))
    quant("SRC", P, 2 * P, "KT")
    mm(0, "QU", 0, "SRC", P, 2 * P)
    copy(quarter("VR", 0), bank(0, 96, 0, 32))
    copy(quarter("VR", 1), bank(0, 96, 32, 64, 96))

    for i in range(4):
        mm(1 + i, "QA", 128 * i, "SRC", P, 2 * P + HN)
    for i in range(4):
        mm((5 + i) % 8, "QB", 128 * i, "SRC", P, 2 * P + HN)
    fill(view("HK", 4 * HN, 4 * P), 0.0)
    for i in range(8):
        e0 = 4 * P * (i // 4)
        copy(view("HK", e0 + i % 4, e0 + 4 * HN, step=4), bank((1 + i) % 8, HN, c0=2 * P), 0.0625)
    for i in range(8):
        e0 = 768 * (i // 4)
        copy(view("GO", e0 + i % 4, e0 + 768, step=4), bank((1 + i) % 8, 2 * P), 0.0625)
    quant("SRC", H0 + P, P + HN, "HK")

    for j in range(N - 1):
        spread(view("EX1", 32 * j, 32 * j + 32), view("X1L", j, j + 1))
    turn(view("R1"), view("EX1"))
    for b in range(2):
        s, o = view("TS", 32 * b, 32 * b + 1), 288 * b
        if r > 0:
            ts(view("CM", o, o + 32 * r), view("R1", 0, 32 * r), s, GE)
            named("GE.%d" % b)
        if r < N - 1:
            ts(view("CM", o + 32 * r, o + 224), view("R1", 32 * r, 224), s, GT)
            named("GT.%d" % b)
        count("CN", 144 * b, view("CM", o, o + 288))
    act(view("TG"), view("R1"), AF.Sign, bias=view("TS", 64, 65), scale=-1.0)
    if r > 0:
        act(waste(view("TG", 0, 32 * r)), view("TG", 0, 32 * r), AF.Relu, acc=view("TA", 0, 1))
        named("TA.0")
    else:
        fill(view("TA", 0, 1), 0.0)
    if r < N - 1:
        act(waste(view("TG", 32 * r, 224)), view("TG", 32 * r, 224), AF.Relu, scale=-1.0, acc=view("TA", 1, 2))
        named("TA.1")
    else:
        fill(view("TA", 1, 2), 0.0)
    ts(view("CN", 431, 432), view("CN", 319, 320), view("TA", 0, 1), SUB, view("TA", 1, 2), ADD)
    for a in (0, 1):
        copy(quarter("CA", a, 0, 3), quarter("CN", 1 - a, 143, 432, 144))
        copy(quarter("CA", a, 3, 6), quarter("CN", 2, 143, 432, 144))
    for b in range(3):
        spread(half("E0", 0, 32 * b, 32 * b + 32), half("CN", 0, 144 * b + 143, 144 * b + 144))
        ts(half("EX3", 0, 32 * b, 32 * b + 32), half("E0", 0, 32 * b, 32 * b + 32), half("CA", 0, b, b + 1), ADD,
           half("CA", 0, 3 + b, 4 + b), ADD)
    turn(half("PR", 0), half("EX3", 0))
    turn(half("PR", 1), half("EX3", 0))
    ts(view("OH"), view("PR"), view("JC"), EQ)
    tt(view("M2"), view("OH"), view("KV"), MUL)
    sums(view("XS", 1, 2), view("M2"))
    tt(view("M1"), view("OH"), view("VR"), MUL)
    sums(view("XS", 0, 1), view("M1"))
    to_all(view("XS"), "X2L", 4, 2, "x2")
    arrive("x2", 7 * lanes, [view("X2L", 4, 18)])

    fill(view("X2L", 2, 4), 0.0)
    copy(view("X2L", 0, 2), view("XS"))
    for i in range(8):
        mm((1 + i) % 8, "QA" if i < 4 else "QB", 128 * (i % 4), "SRC", H0 + P, P + HN)
    quant("SRC", AA * P, 2 * P, "GO")
    quant("SRC", BA * P, 2 * P, "GO", 768)
    for h in range(2):
        ts(view("PC", h, h + 1), view("PB"), 16.0 * h, ADD, E - 1.0, MIN)
    swap("WC", 4, True)
    act(view("P2"), view("PC"), bias=2.0 * E * r, scale=2.0)
    act(view("PN"), view("PC"), bias=2.0 * E * r + 2.0, scale=2.0)
    act(view("NN"), view("PC", 1, 2), bias=-2.0 * E * r - 2.0, scale=-2.0)
    act(view("NS"), view("PC"), bias=-2.0 * E * r - 1.0, scale=-2.0)
    act(view("W", 256, 528, step=264), view("PC"), bias=2.0 * E * r - 128.0 - 2.0 * P * r, scale=2.0)
    act(view("W", 260, 528, step=264), view("PC"), bias=2.0 * E * r - 128.0 - 2.0 * P * (r + 1), scale=2.0)
    act(view("H2"), view("PF"), bias=2.0 * E * r, scale=2.0)
    act(view("NH"), view("PF"), bias=-2.0 * E * r - 1.0, scale=-2.0)
    act(view("WH", 128, 129), view("PF"), bias=4.0 * E * r - 256.0, scale=4.0)
    if r == 0:
        fill(view("W", 258, 528, step=264), 0.0)
    if r == N - 1:
        fill(view("W", 259, 528, step=264), 0.0)
    quant("QW", 0, 128, "WT")
    for i in range(8):
        e0 = 672 * (i // 4)
        copy(view("HG", e0 + i % 4, e0 + 672, step=4), bank((1 + i) % 8, P + HN), 0.0625)
    quant("SRC", H0 + AA * P, P + HN, "HG")
    quant("SRC", H0 + BA * P, P + HN, "HG", 672)

    sc, mc = view("EX2", 0, 1), view("EX2", 64, 65)
    for k, row in ((0, "DS"), (1, "DN")):
        sums(view("SC", k, k + 1), view("X2L", k, 18, step=2))
        spread(view("EX2", 64 * k, 64 * k + 32), view("SC", k, k + 1))
        for h in (0, 1):
            spread(half("EX2", h, 64 * k + 32, 64 * k + 64), half("SC", 1 - h, k, k + 1))
        turn(view(row, 0, 64), view("EX2", 64 * k, 64 * k + 64))
        swap(row, 32)
    act(view("SG"), view("DS"), AF.Sign, bias=sc, scale=-1.0)
    ts(view("LO"), view("DN"), mc, GE, -0.5, MUL)
    tt(view("BF"), view("SG"), view("LO"), LE)
    count("P1", 0, view("BF"))
    ts(view("EXM"), view("THR"), view("P1", 63, 64), ADD, mc, MAX)
    turn(view("MR", 0, 32), view("EXM"))
    for h in (0, 1):
        turn(half("MR", h, 32, 64), half("EXM", 1 - h))
    swap("MR", 32)
    signs(view("MR"), view("EXM", 0, 1), view("RK"), -1.0)
    ts(view("F0"), view("EXM", 0, 1), 0.5 / UNIT, MUL, view("FC"), ADD)
    spread(view("F32"), view("F0"))
    if r > 0:
        signs(view("MR"), (4.0 * P * r - 0.5) * UNIT, view("SB", 0, 1), -1.0)
    if r < N - 1:
        signs(view("MR"), (4.0 * P * (r + 1) - 0.5) * UNIT, view("SB", 1, 2), -1.0)
    spread(view("EXF", 0, 32), view("RK"), view("F32"))
    for h in (0, 1):
        spread(half("EXF", h, 32, 64), half("RK", 1 - h), half("F32", 1 - h))
    turn(view("FR", 0, 64), view("EXF"))
    swap("FR", 32)

    for h in range(2):
        signs(view("FR"), view("NS", h, h + 1), view("W", 264 * h + 257, 264 * h + 258))
    act(view("AB"), view("FR"), AF.Abs, bias=view("NN"))
    for k in range(4):
        c = 264 + 128 + 32 * k
        act(view("W", c, c + 32), view("AB", 32 * k, 32 * k + 32), AF.Relu, bias=view("WC", 4 * k + 1, 4 * k + 2), scale=view("WC", 4 * k + 3, 4 * k + 4))
    if r > 0:
        ts(view("W", 258, 528, step=264), view("W", 256, 528, step=264), view("SB", 0, 1), LT, 2.0 * (H0 + 64 - 8 * r), MUL)
        named("low")
    if r < N - 1:
        ts(view("W", 259, 528, step=264), view("W", 260, 528, step=264), view("SB", 1, 2), GE, 2.0 * (H0 - 32 - 8 * r), MUL)
        named("high")
    for h in range(2):
        for k in range(4):
            f, c = view("FR", 32 * k, 32 * k + 32), 264 * h + 32 * k
            ts(view("W", c, c + 32), f, view("P2", h, h + 1), EQ, view("WC", 4 * k, 4 * k + 1), MUL)
            if h == 0:
                ts(view("W", c + 128, c + 160), f, view("PN", h, h + 1), EQ, view("WC", 4 * k + 1, 4 * k + 2), MUL)
    for h in range(2):
        count("OF", 130 * h, view("W", 264 * h, 264 * h + 260))
    for a in range(4):
        for b in range(4):
            copy(quarter("OTF", b, 2 * a, 2 * a + 2), quarter("OF", a, 129, 260, 130))
    ts(view("OT"), view("OTF"), 0.5, MUL)
    op("v", lambda e, q: e.tensor_copy(T.RUN[:, 0:128].bitcast(dt.uint32), T.SRC[:, 0:ALL].bitcast(dt.uint32).indirect(T.OT[:, 0:8])),
       [view("SRC"), view("OT")], [view("RUN")], 0.26)
    op("s", lambda e, q: e.activation(T.sRUN[:, 0:128], T.sSRC[:, 0:ALL].indirect(T.OT[:, 0:8]), AF.Copy),
       [view("sSRC"), view("OT")], [view("sRUN")], 0.28)

    mm(0, "QW", 0, "RUN", 0, 128)
    copy(view("YT"), bank(0, E))
    store(lambda e: e.dma_start(T.y[:, 0:E], T.YT[:]), view("YT"), "o5")
    store(lambda e: e.dma_start(T.oc[:, 0:4 * E], T.RUN[:, 0:E].bitcast(dt.uint8)), view("RUN", 0, E), "o0")
    for k in range(4):
        store(lambda e, k=k: e.dma_start(T.osc[4 * k:4 * k + 4, 0:E], T.sRUN[32 * k:32 * k + 4, 0:E]), view("sRUN", 0, E, 32 * k, 32 * k + 4), "o%d" % (1 + k))
    for k in (129, 130):
        signs(view("FR"), view("NH"), view("WH", k, k + 1))
    for k in range(4):
        ts(view("WH", 32 * k, 32 * k + 32), view("FR", 32 * k, 32 * k + 32), view("H2"), EQ, view("WC", 4 * k + 2, 4 * k + 3), MUL)
    sums(view("HB"), view("WH", 0, 131))
    store(lambda e: e.dma_start(T.hs[0:1, 0:E], T.HB[0:E, 0:1]), view("HB", 0, 1, 0, E), "o6")

    order, queue = place(ops, *links(ops), ORDER)
    total = {}
    known = {k: {} for k in queues}
    clocks = {}
    log = {}

    def await_(q, need):
        for s, n in sorted(need.items()):
            if known[q].get(s, 0) < n:
                queues[q].wait_ge(T.sem[s], n)
                for s2, n2 in clocks.get((s, n), {}).items():
                    known[q][s2] = max(known[q].get(s2, 0), n2)
                known[q][s] = n

    for i in order:
        o, q = ops[i], queue[i]
        sem = o["sem"] or q
        if o["fn"] is not None:
            need = {}
            for w, wr in accesses(o):
                for v, vr, s, n, q2 in log.get(w[0], []):
                    if (wr or vr or (w[0] == "ps" and q2 != q)) and meet(wide(w), v):
                        need[s] = max(need.get(s, 0), n)
            await_(q, need)
            ins = o["fn"](queues[q], q)
            if o["local"]:
                ins.then_inc(T.sem[sem], o["inc"])
            total[sem] = total.get(sem, 0) + o["inc"]
            clocks[(sem, total[sem])] = dict(known[q])
        else:
            total[sem] = o["inc"]
        for w, wr in accesses(o):
            w = wide(w)
            l = log.setdefault(w[0], [])
            if wr:
                l[:] = [e for e in l if not holds(w, e[0])]
            l.append((w, wr, sem, total[sem], q))
    await_("y", total)
